import numpy as np, ml_dtypes
CORES = [3,11,19,27,35,43,51,59]
N = 8
BF = ml_dtypes.bfloat16
def gentries(a):
    return np.ascontiguousarray(a.reshape(8, 16, -1).transpose(0, 2, 1)).reshape(8, -1)
def gtable(e):
    e = np.asarray(e); return np.ascontiguousarray(e.reshape(8, -1, 16).transpose(0, 2, 1)).reshape(128, -1).astype(np.int32)
M, D, L, Q = 8192, 3, 2, 2048
S = [0, 8192, 12288, 14336, 15360]
NODES = S[-1]; FULL = 2 ** L - 1; QP = Q // N
def gtables(a):
    return np.stack([gtable(e) for e in a])
def letters(rng, *shape):
    return np.left_shift(np.uint8(1), rng.integers(0, L, shape, dtype=np.uint8))
def anyset(rng, *shape):
    return rng.integers(1, FULL + 1, shape, dtype=np.uint8)
def tobf(v):
    return v.astype(np.float32).astype(BF)
def pairs(rng):
    le = np.zeros((N, 8, NODES - M), np.int64); ri = le.copy()
    for d in range(1, D + 1):
        e = S[d - 1] + np.argsort(rng.random((N, 8, S[d] - S[d - 1])), axis=2); a, b = S[d] - M, S[d + 1] - M
        le[:, :, a:b] = e[:, :, 0::2]; ri[:, :, a:b] = e[:, :, 1::2]
    return le, ri
def nodes(rng):
    d = rng.integers(0, D + 1, (N, 8, Q)); lo = np.array(S)[d]; n = np.array(S)[d + 1] - lo
    return lo + np.minimum((rng.random((N, 8, Q)) * n).astype(np.int64), n - 1)
def setup_inputs(rng):
    le, ri = pairs(rng)
    leaf = np.where(rng.random((N, 128, M), dtype=np.float32) < 0.125, anyset(rng, N, 128, M), letters(rng, N, 128, M))
    return {"leaf": tobf(leaf), "left": gtables(le), "right": gtables(ri), "clade": gtables(nodes(rng)), "edge": gtables(nodes(rng))}
def setup_inputs_near(rng):
    d = setup_inputs(rng); rate = np.repeat(0.1 * (1 + np.arange(8)), 16).reshape(1, 128, 1).astype(np.float32)
    leaf = np.where(rng.random((N, 128, M), dtype=np.float32) < rate, d["leaf"].astype(np.float32), letters(rng, 1, 128, 1).astype(np.float32))
    d["leaf"] = tobf(leaf); return d
def setup_inputs_order(rng):
    d = setup_inputs(rng); le = np.zeros((N, 8, NODES - M), np.int64); ri = le.copy()
    for k in range(1, D + 1):
        e = np.arange(S[k - 1], S[k]); a, b = S[k] - M, S[k + 1] - M
        le[0::2, :, a:b] = e[0::2]; ri[0::2, :, a:b] = e[1::2]
        le[1::2, :, a:b] = e[::-1][0::2]; ri[1::2, :, a:b] = e[::-1][1::2]
    d["left"] = gtables(le); d["right"] = gtables(ri)
    j = np.broadcast_to(np.arange(Q), (N, 8, Q))
    d["edge"] = gtables(j); d["clade"] = gtables(NODES - 1 - j); return d
def setup_inputs_few(rng):
    d = setup_inputs(rng); p = np.array([0, M - 1, M, S[D], NODES - 1])
    d["clade"] = gtables(p[rng.integers(0, 5, (N, 8, Q))]); d["edge"] = gtables(p[rng.integers(0, 5, (N, 8, Q))]); return d
def setup_inputs_far(rng):
    d = setup_inputs_order(rng); h = M // 2
    a = rng.integers(0, L, (1, 128, 1)); b = (a + rng.integers(1, L, (1, 128, 1))) % L
    leaf = np.where(np.arange(M) < h, np.left_shift(1, a), np.left_shift(1, b))
    d["leaf"] = tobf(np.repeat(leaf, N, axis=0))
    c = rng.integers(h, M, (N, 8, Q)); mv = (rng.random((N, 8, Q)) < 0.125) & (np.arange(8).reshape(1, 8, 1) >= 4)
    d["clade"] = gtables(np.where(mv, c - h, c)); d["edge"] = gtables(rng.integers(0, h, (N, 8, Q))); return d
def setup_inputs_spread(rng):
    d = setup_inputs(rng); p = rng.random((N, 128, L)) ** 3 + 1e-6; c = np.add.accumulate(p, axis=2); c = (c / c[:, :, -1:]).astype(np.float32)
    x = rng.random((N, 128, M), dtype=np.float32); lt = np.zeros((N, 128, M), np.uint8)
    for k in range(L - 1): lt += x > c[:, :, k:k + 1]
    am = rng.choice(np.array([0, 0, 0, 0.02, 0.02, 1], np.float32), (N, 1, M))
    amb = np.where(rng.random((N, 128, M), dtype=np.float32) < 0.5, np.uint8(FULL), anyset(rng, N, 128, M))
    d["leaf"] = tobf(np.where(rng.random((N, 128, M), dtype=np.float32) < am, amb, np.left_shift(np.uint8(1), lt)))
    e = np.minimum((NODES * rng.random((N, 8, Q)) ** 4).astype(np.int64), NODES - 1); h = np.minimum((NODES * rng.random((N, 8, Q)) ** 4).astype(np.int64), NODES - 1)
    d["edge"] = gtables(e); d["clade"] = gtables(NODES - 1 - h); return d
def check_inputs(d):
    bad = []
    try:
        v = d["leaf"].astype(np.float32)
        if not ((v == np.floor(v)) & (v >= 1) & (v <= FULL)).all(): bad.append("leaf")
        ok = True
        for q in range(N):
            le, ri = gentries(d["left"][q]), gentries(d["right"][q])
            for k in range(1, D + 1):
                a, b = S[k] - M, S[k + 1] - M
                e = np.sort(np.concatenate([le[:, a:b], ri[:, a:b]], axis=1), axis=1)
                ok = ok and bool((e == np.arange(S[k - 1], S[k])).all())
        if not ok: bad.append("left and right")
        for a in ("clade", "edge"):
            if not ((d[a] >= 0) & (d[a] < NODES)).all(): bad.append(a)
    except Exception:
        bad.append("shapes")
    return bad
def fitch(a, b):
    i = a & b
    return np.where(i > 0, i, a | b)
def reference(leaf, left, right, clade, edge):
    inside = np.zeros((N, 8, 16, NODES), np.uint8); outside = np.full((N, 8, 16, NODES), FULL, np.uint8)
    inside[:, :, :, :M] = leaf.astype(np.float32).astype(np.uint8).reshape(N, 8, 16, M)
    for q in range(N):
        le, ri = gentries(left[q]), gentries(right[q])
        for g in range(8):
            u, o = inside[q, g], outside[q, g]
            for d in range(1, D + 1):
                x, z = le[g, S[d] - M:S[d + 1] - M], ri[g, S[d] - M:S[d + 1] - M]
                u[:, S[d]:S[d + 1]] = fitch(u[:, x], u[:, z])
            for d in range(D, 0, -1):
                x, z = le[g, S[d] - M:S[d + 1] - M], ri[g, S[d] - M:S[d + 1] - M]
                o[:, x] = fitch(o[:, S[d]:S[d + 1]], u[:, z])
                o[:, z] = fitch(o[:, S[d]:S[d + 1]], u[:, x])
    on = fitch(inside, outside); c = np.zeros((N, 8, Q), np.int64)
    for r in range(N):
        cl, ed = gentries(clade[r]), gentries(edge[r])
        for g in range(8):
            for q in range(N):
                j = slice(q * QP, (q + 1) * QP)
                c[r, g, j] = np.sum((inside[q, g][:, cl[g, j]] & on[r, g][:, ed[g, j]]) == 0, axis=0)
    runs = c.reshape(N, 8, 8, Q // 8)
    return {"cost": np.min(runs, axis=2).astype(np.float32), "first": np.argmin(runs, axis=2).astype(np.float32)}

@@ -1,0 +1,405 @@
+from concourse.bass import DstId, RemoteDMATransfer
+from concourse.mybir import AluOpType as ALU, ActivationFunctionType as ACT
+
+N = 8
+M, N1, N2, N3 = 8192, 4096, 2048, 1024
+Q, QP = 2048, 256
+PAD = 16
+Z1, Z2, Z3, ZE = PAD, PAD + N1, PAD + N1 + N2, PAD + N1 + N2 + N3
+L1, L2, L3, R1, R2, R3 = 0, 256, 384, 448, 704, 832
+CUT = {
+    "s_par": 1024,
+    "v_mid": 1280,
+    "lev1": (0, 1024, 2048, 3072, 3584, 4096),
+    "pe1": 512,
+    "v2": 1024,
+    "vo": 1024,
+    "qa0": 512,
+    "late": "copla",
+    "wl": 3584,
+    "vx": 1,
+    "so": 1,
+}
+
+SCRATCH = {
+    "leafs": ("sbuf", [128, M + PAD], "bfloat16"),
+    "kid32": ("sbuf", [128, 896], "int32"),
+    "kid": ("sbuf", [128, 896], "uint16"),
+    "edg32": ("sbuf", [128, 128], "int32"),
+    "cla32": ("sbuf", [128, 128], "int32"),
+    "ask32": ("sbuf", [128, 128], "int32"),
+    "eleaf": ("sbuf", [128, 128], "uint16"),
+    "ebase": ("sbuf", [128, 128], "float32"),
+    "wlist": ("sbuf", [128, 128], "uint16"),
+    "slist": ("sbuf", [128, 128], "uint16"),
+    "aleaf": ("sbuf", [128, 128], "uint16"),
+    "ainner": ("sbuf", [128, 128], "uint16"),
+    "cnt": ("sbuf", [128, N2], "float32"),
+    "par": ("sbuf", [128, M + PAD], "float32"),
+    "sib2": ("sbuf", [128, N2], "float32"),
+    "look": ("sbuf", [128, Q], "float32"),
+    "a1": ("sbuf", [128, N1 + 1024], "bfloat16"),
+    "a2": ("sbuf", [128, N1], "bfloat16"),
+    "a3": ("sbuf", [128, N2], "bfloat16"),
+    "o2m": ("sbuf", [128, N2], "bfloat16"),
+    "zin": ("sbuf", [128, ZE], "bfloat16"),
+    "zout": ("sbuf", [128, ZE], "bfloat16"),
+    "cl_s": ("sbuf", [128, Q], "bfloat16"),
+    "ci_s": ("sbuf", [128, Q], "bfloat16"),
+    "cl_r": ("sbuf", [128, Q], "bfloat16"),
+    "ci_r": ("sbuf", [128, Q], "bfloat16"),
+    "qa": ("sbuf", [128, Q], "bfloat16"),
+    "qx": ("sbuf", [128, Q], "bfloat16"),
+    "qo": ("sbuf", [128, Q], "bfloat16"),
+    "mag": ("sbuf", [128, Q], "bfloat16"),
+    "ind": ("sbuf", [128, 8, 16, 16], "float16"),
+    "ones": ("sbuf", [128, 128], "float32"),
+    "idf": ("sbuf", [128, 128], "float32"),
+    "id1": ("sbuf", [128, 128], "bfloat16"),
+    "idm": ("sbuf", [128, 128], "bfloat16"),
+    "sel": ("sbuf", [128, 16], "float32"),
+    "bf": ("sbuf", [128, 144], "float32"),
+    "bh": ("sbuf", [128, 144], "float16"),
+    "kt": ("sbuf", [128, 128], "bfloat16"),
+    "m48": ("sbuf", [128, 48], "float32"),
+    "n48": ("sbuf", [128, 48], "float32"),
+    "n16": ("sbuf", [128, 48], "float32"),
+    "key": ("sbuf", [128, 16], "int32"),
+    "res32": ("sbuf", [128, 32], "int32"),
+    "res": ("sbuf", [128, 32], "float32"),
+    "p0": ("psum", [128, 512], "float32"),
+    "p1": ("psum", [128, 512], "float32"),
+    "p2": ("psum", [128, 512], "float32"),
+    "p3": ("psum", [128, 512], "float32"),
+    "ps": ("psum", [128, 512], "float32"),
+    "pw": ("psum", [128, 512], "float32"),
+    "pk": ("psum", [128, 512], "float32"),
+    "pl": ("psum", [128, 512], "float32"),
+}
+NDMA = 18
+SEMAPHORES = ["cv", "cs", "ct", "cg", "sent", "got_ask", "got_cl", "got_ci"] + ["d%d" % i for i in range(NDMA)]
+PSUM = ("p0", "p1", "p2", "p3", "ps", "pw", "pk", "pl")
+
+
+def _plan(g, core, T, topo, rank):
+    ops = []
+
+    def add(q, kind, fn, rd, wr):
+        ops.append((q, kind, fn, rd, wr))
+
+    def V(fn, rd, wr): add("v", "c", fn, rd, wr)
+    def S(fn, rd, wr): add("s", "c", fn, rd, wr)
+    def G(fn, rd, wr): add("g", "c", fn, rd, wr)
+    def P(fn, rd, wr): add("t", "c", fn, rd, wr)
+    def D(q, fn, rd, wr): add(q, "d", fn, rd, wr)
+
+    def ap(r): return T[r[0]][:, r[1]:r[2]]
+    def ind(win, off): return ap(win).indirect(ap(off))
+
+    def vfill(r, c): V(lambda: g.vector.memset(ap(r), c), [], [r])
+    def vts(o, i, s1, s2, op0, op1=None):
+        if op1 is None: V(lambda: g.vector.tensor_scalar(ap(o), ap(i), s1, None, op0), [i], [o])
+        else: V(lambda: g.vector.tensor_scalar(ap(o), ap(i), s1, s2, op0, op1), [i], [o])
+    def vcopy(o, i): V(lambda: g.vector.tensor_copy(ap(o), ap(i)), [i], [o])
+    def vtt(o, a, b, op): V(lambda: g.vector.tensor_tensor(ap(o), ap(a), ap(b), op), [a, b], [o])
+    def vget2(o, win, off, s1, s2, op0, op1):
+        V(lambda: g.vector.tensor_scalar(ap(o), ind(win, off), s1, s2, op0, op1), [win, off], [o])
+    def vget(o, win, off): V(lambda: g.vector.tensor_copy(ap(o), ind(win, off)), [win, off], [o])
+    def sget(o, win, off, f, bias=0.0, scale=1.0):
+        S(lambda: g.scalar.activation(ap(o), ind(win, off), f, bias=bias, scale=scale), [win, off], [o])
+    def sput(win, off, src):
+        S(lambda: g.scalar.activation(ind(win, off), ap(src), ACT.Silu), [off, src], [win])
+    def sact(o, i, f, bias=0.0): S(lambda: g.scalar.activation(ap(o), ap(i), f, bias=bias), [i], [o])
+    def mm(o, w, x, start, stop, xap=None):
+        P(lambda: g.tensor.matmul(ap(o), ap(w), ap(x) if xap is None else xap, start, stop), [w, x], [o])
+    def cols(base, a, b): return ("kid", base + a // 16, base + b // 16)
+    def load(q, dst, src):
+        D(q, lambda: (g.sync if q == "y" else g.scalar).dma_start(ap(dst), src), [], [dst])
+    def count_up(a, b):
+        G(lambda: g.iota(T.cnt[:, a:b], [[1, b - a]], PAD + a, 0, allow_small_or_imprecise_dtypes=True), [], [("cnt", a, b)])
+
+    def send(src, dst, w, sem):
+        def fn():
+            tr, used = [], []
+            for s in range(1, N):
+                q = (rank + s) % N
+                to = T.cores[q]
+                e = [x for x in topo.engines(core, to) if x not in used][0]
+                used.append(e)
+                rid, pid, _ = topo.addr(to)
+                tr.append(RemoteDMATransfer(dst_ids=[DstId(rid=rid, pnc=pid)], dma_engine_mask=1 << e, remote_sem=T.sem[sem],
+                                            src=T[src][:, q * w:(q + 1) * w], dst=T[dst][:, rank * w:(rank + 1) * w]))
+            return g.remote_dma_fused(tr, local_sem=T.sem.sent)
+        others = [q for q in range(N) if q != rank]
+        add("g", "r", fn, [(src, q * w, (q + 1) * w) for q in others], [])
+        add(None, sem, None, [], [(dst, q * w, (q + 1) * w) for q in others])
+
+    LEAF, PAR, ZIN, ZOUT = ("leafs", 0, M + PAD), ("par", 0, M + PAD), ("zin", 0, ZE), ("zout", 0, ZE)
+    PAR0, SIB = ("par", 0, M), ("sib2", 0, N2)
+    W1, W2 = ("zin", Z1, Z2), ("zin", Z2, Z3)
+
+    def leaf(o, off): sget(o, LEAF, off, ACT.Abs, -4.5, 2.0)
+    def edge_leaf(a, b): sget(("qa", a, b), LEAF, ("eleaf", a // 16, b // 16), ACT.Abs, -2.25, 1.0)
+
+    def vpar(base, a, b):
+        while a < b:
+            e = min(b, a + N2)
+            off, src = cols(base, a, e), ("cnt", 0, e - a)
+            V(lambda off=off, src=src, a=a: g.vector.tensor_scalar(ind(PAR0, off), ap(src), 1.0, float(a), ALU.mult, ALU.add), [off, src], [PAR0])
+            a = e
+
+    def to_list(pb, src, c0, c1, extra):
+        o, x = (pb, c0, c1), (src, 16 * c0, 16 * c1)
+        if extra is not None:
+            mm(o, ("idf", 0, 128), (extra, c0, c1), True, False)
+        for s in range(16):
+            mm(o, ("bf", 15 - s, 143 - s), x, s == 0 and extra is None, s == 15, xap=T[src][:, 16 * c0 + s:16 * c1:16])
+
+    def answer(name, lst, win, f, bias, scale, sem):
+        for a, b in ((0, rank), (rank + 1, N)):
+            if b > a:
+                sget((name + "_s", QP * a, QP * b), win, (lst, 16 * a, 16 * b), f, bias, scale)
+        send(name + "_s", name + "_r", QP, sem)
+        sget((name + "_r", QP * rank, QP * rank + QP), win, (lst, 16 * rank, 16 * rank + 16), f, bias, scale)
+
+    load("s", ("kid32", R3, 896), T.right[:, L3:R1])
+    load("y", ("kid32", L1, L2), T.left[:, L1:L2])
+    load("s", ("kid32", L3, R1), T.left[:, L3:R1])
+    load("y", ("kid32", R1, R2), T.right[:, L1:L2])
+    load("y", ("leafs", 0, M), T.leaf[:])
+    load("y", ("cla32", 0, 128), T.clade[:])
+    load("y", ("kid32", L2, L3), T.left[:, L2:L3])
+    load("y", ("kid32", R2, R3), T.right[:, L2:L3])
+    load("y", ("edg32", 0, 128), T.edge[:])
+    vfill(("ones", 0, 128), 1.0)
+    vfill(("bf", 0, 144), 0.0)
+    vfill(("leafs", M, M + PAD), 3.0)
+    vfill(("zin", 0, PAD), 3.0)
+    vfill(("zout", 0, PAD), 0.0)
+    vfill(("zout", Z3, ZE), 0.0)
+    vfill(("par", M, M + PAD), float(PAD - 1))
+    count_up(0, 512)
+    sact(("cnt", 512, 1024), ("cnt", 0, 512), ACT.Silu, 512.0)
+    G(lambda: g.affine_select(T.sel[:, 0:8], T.ones[:, 0:8], [[-16, 8]], ALU.is_ge, 0.0, 0, 1), [("ones", 0, 8)], [("sel", 0, 8)])
+    G(lambda: g.affine_select(T.sel[:, 8:16], T.sel[:, 0:8], [[16, 8]], ALU.is_ge, 0.0, 15, -1), [("sel", 0, 8)], [("sel", 8, 16)])
+    G(lambda: g.affine_select(T.idf[:], T.ones[:], [[-1, 128]], ALU.is_equal, 0.0, 0, 1), [("ones", 0, 128)], [("idf", 0, 128)])
+    count_up(1024, 2048)
+    G(lambda: g.iota(T.kt[:], [[1, 8], [0, 16]], 0, 0, allow_small_or_imprecise_dtypes=True), [], [("kt", 0, 128)])
+    vts(("kid", R3, 896), ("kid32", R3, 896), float(-(M + N1)), None, ALU.add)
+    vts(("kid", L3, R1), ("kid32", L3, R1), float(-(M + N1)), None, ALU.add)
+    vcopy(("kid", L1, L2), ("kid32", L1, L2))
+    sput(SIB, cols(R3, 0, N3), ("cnt", 0, N3))
+    sput(SIB, cols(L3, 0, N3), ("cnt", N3, N2))
+    vpar(L1, 0, 1024)
+    vcopy(("kid", R1, R2), ("kid32", R1, R2))
+    V(lambda: g.vector.tensor_scalar(T.bf[:, 15:143:16], T.sel[:, 8:16], 1.0 / 16, None, ALU.mult), [("sel", 8, 16)], [("bf", 0, 144)])
+    vcopy(("id1", 0, 128), ("idf", 0, 128))
+    vts(("idm", 0, 128), ("idf", 0, 128), -4.0, None, ALU.mult)
+    vcopy(("bh", 0, 144), ("bf", 0, 144))
+    vpar(L1, 1024, 2048)
+    send("cla32", "ask32", 16, "got_ask")
+    to_list("ps", "sib2", 0, 128, None)
+    vpar(L1, 2048, 3072)
+    vts(("kid", L2, L3), ("kid32", L2, L3), float(-M), None, ALU.add)
+    vts(("kid", R2, R3), ("kid32", R2, R3), float(-M), None, ALU.add)
+    vts(("eleaf", 0, 128), ("edg32", 0, 128), float(M), None, ALU.min)
+    vts(("ebase", 0, 128), ("edg32", 0, 128), float(1 - M), 0.0, ALU.add, ALU.max)
+    vcopy(("ask32", 16 * rank, 16 * rank + 16), ("cla32", 16 * rank, 16 * rank + 16))
+    vpar(L1, 3072, 4096)
+    vts(("aleaf", 0, 128), ("ask32", 0, 128), float(M), None, ALU.min)
+    vts(("ainner", 0, 128), ("ask32", 0, 128), float(PAD - M), 0.0, ALU.add, ALU.max)
+    vts(("slist", 0, 128), ("ps", 0, 128), 0.25 - PAD, None, ALU.add)
+    vpar(R1, CUT["s_par"] + CUT["v_mid"], N1)
+
+    cuts = CUT["lev1"]
+    for a, b in zip(cuts[:-1], cuts[1:]):
+        src, dst = ("a1", a, b), ("zin", Z1 + a, Z1 + b)
+        if a >= N1 - CUT["pe1"]:
+            bank, left = ("pk" if b == N1 else "pl", 0, b - a), ("a1", N1 + a % 1024, N1 + a % 1024 + b - a)
+            leaf(left, cols(L1, a, b))
+            leaf(src, cols(R1, a, b))
+            mm(bank, ("id1", 0, 128), left, True, False)
+            mm(bank, ("id1", 0, 128), src, False, True)
+            vcopy(dst, bank)
+        else:
+            leaf(dst, cols(L1, a, b))
+            leaf(src, cols(R1, a, b))
+            D("g", lambda src=src, dst=dst: g.dma_start(ap(dst), ap(src), accum_op=ALU.add), [src, dst], [dst])
+    answer("cl", "aleaf", LEAF, ACT.Abs, -4.5, 2.0, "got_cl")
+
+    def gather(tab, n, h, lb, rb, win):
+        for base, o in ((lb, 0), (rb, n)):
+            if h:
+                vget2((tab, o, o + h), win, cols(base, 0, h), 2.0, 4.0, ALU.max, ALU.min)
+            sget((tab, o + h, o + n), win, cols(base, h, n), ACT.Sign, -3.0)
+    def sums(tab, n, banks, order):
+        for o in (0, n):
+            for b in order:
+                mm((banks[b], 0, 512), ("id1", 0, 128), (tab, o + 512 * b, o + 512 * b + 512), o == 0, o == n)
+    def evac(z, h, banks, order, on):
+        for b in order:
+            m = min(512, max(0, h - 512 * b))
+            for x, y, c in ((0, m, -3.0), (m, 512, 3.0)):
+                if y > x:
+                    dst = ("zin", z + 512 * b + x, z + 512 * b + y)
+                    if on[b] == "v": vts(dst, (banks[b], x, y), c, None, ALU.add)
+                    else: sact(dst, (banks[b], x, y), ACT.Identity, c)
+
+    v2, vo, qa0 = CUT["v2"], CUT["vo"], CUT["qa0"]
+    ub = ["p0", "p1", "p2", "p3"]
+    gather("a2", N2, v2, L2, R2, W1)
+    if qa0:
+        edge_leaf(0, qa0)
+    sums("a2", N2, ub, (0, 2, 1, 3))
+    evac(Z2, v2, ub, (0, 2, 1, 3), "vvss")
+    vpar(R1, CUT["s_par"], CUT["s_par"] + CUT["v_mid"])
+    gather("a3", N3, 0, L3, R3, W2)
+    sums("a3", N3, ["pk", "pl"], (0, 1))
+    A3 = ("a3", 0, N2)
+    vget(("zout", Z2, Z2 + vo), A3, ("slist", 0, vo // 16))
+    def term(b, w, name, start=False, stop=False):
+        mm((ub[b], 0, 512), (w, 0, 128), (name, 512 * b, 512 * b + 512), start, stop)
+    for b in range(4):
+        term(b, "idm", "cl_r", start=True)
+    for c in CUT["late"]:
+        if c == "c":
+            evac(Z3, 0, ["pk", "pl"], (0, 1), "ss")
+            answer("ci", "ainner", ZIN, ACT.Sign, -3.0, 1.0, "got_ci")
+        if c == "o":
+            for a in range(vo, N2, 512):
+                b = min(N2, a + 512)
+                sget(("zout", Z2 + a, Z2 + b), A3, ("slist", a // 16, b // 16), ACT.Identity)
+        if c == "p" and CUT["s_par"]:
+            sput(PAR0, cols(R1, 0, CUT["s_par"]), ("cnt", 0, CUT["s_par"]))
+        if c == "l":
+            for c0 in (0, 64):
+                sget(("look", 16 * c0, 16 * c0 + 1024), PAR, ("eleaf", c0, c0 + 64), ACT.Identity)
+                to_list("pw", "look", c0, c0 + 64, "ebase")
+        if c == "a" and qa0 < Q:
+            edge_leaf(qa0, Q)
+
+    O1 = ("zout", Z1, Z2)
+    done = 0
+    pcut = sorted(set([0, min(vo, v2), v2, N2] + list(range(0, N2, 512))))
+    for a, b in zip(pcut[:-1], pcut[1:]):
+        x = ("zout", Z2 + a, Z2 + b)
+        if b <= v2:
+            vts(("o2m", a, b), x, -3.0, None, ALU.add)
+            x = ("o2m", a, b)
+        for base, o in ((L2, N2), (R2, 0)):
+            off, y = cols(base, a, b), ("a2", o + a, o + b)
+            V(lambda off=off, x=x, y=y: g.vector.tensor_tensor(ind(O1, off), ap(x), ap(y), ALU.add), [off, x, y], [O1])
+            if done < CUT["wl"] <= done + b - a:
+                vts(("wlist", 0, 128), ("pw", 0, 128), 0.25, None, ALU.add)
+            done += b - a
+
+    def wl(b): return ("wlist", 32 * b, 32 * b + 32)
+    def blk(name, b): return (name, 512 * b, 512 * b + 512)
+    vx, so = CUT["vx"], CUT["so"]
+    for b in range(4):
+        term(b, "id1", "qa")
+    for b in range(4 - vx):
+        sget(blk("qx", b), ZIN, wl(b), ACT.Identity, -2.25, 0.75)
+        term(b, "id1", "qx")
+        term(b, "idm", "ci_r")
+    for b in range(4 - vx, 4):
+        term(b, "idm", "ci_r")
+    for b in range(so):
+        sget(blk("qo", b), ZOUT, wl(b), ACT.Sign)
+    for b in range(so, 4):
+        vget2(blk("qo", b), ZOUT, wl(b), -1.0, 1.0, ALU.max, ALU.min)
+        if b >= 4 - vx:
+            vget2(blk("qx", b), ZIN, wl(b), 0.75, -2.25, ALU.mult, ALU.add)
+    for b in range(4):
+        if b >= 4 - vx:
+            term(b, "id1", "qx")
+        term(b, "id1", "qo", stop=True)
+    for b in range(4):
+        sact(blk("mag", b), (ub[b], 0, 512), ACT.Abs, 5.25)
+    for pb, k0, k1 in (("pk", 0, 6), ("pl", 6, 8)):
+        for b in range(k0 // 2, k1 // 2):
+            V(lambda b=b: g.vector.tensor_scalar(T.ind[:, 2 * b:2 * b + 2, :, :], T.mag[:, 512 * b:512 * b + 512], 4.625, 128.0, ALU.is_ge, ALU.mult),
+              [blk("mag", b)], [blk("ind", b)])
+        o = (pb, 0, 16 * (k1 - k0))
+        mm(o, ("id1", 0, 128), ("kt", 16 * k0, 16 * k1), True, False)
+        for h in range(16):
+            mm(o, ("bh", 15 - h, 143 - h), ("ind", QP * k0, QP * k1), False, h == 15, xap=T.ind[:, k0:k1, h, :])
+    vcopy(("m48", 0, 48), ("pk", 0, 48))
+    vtt(("n48", 0, 48), ("pk", 48, 96), ("m48", 0, 48), ALU.min)
+    vtt(("n16", 0, 16), ("n48", 0, 16), ("n48", 16, 32), ALU.min)
+    vtt(("n16", 16, 32), ("pl", 0, 16), ("n48", 32, 48), ALU.min)
+    vtt(("n16", 32, 48), ("pl", 16, 32), ("n16", 0, 16), ALU.min)
+    vtt(("key", 0, 16), ("n16", 16, 32), ("n16", 32, 48), ALU.min)
+    vts(("res32", 0, 16), ("key", 0, 16), 3, None, ALU.arith_shift_right)
+    vts(("res32", 16, 32), ("key", 0, 16), 7, None, ALU.bitwise_and)
+    vcopy(("res", 0, 32), ("res32", 0, 32))
+    D("y", lambda: g.sync.dma_start(T.cost[:], T.res[:, 0:16]), [("res", 0, 16)], [])
+    D("s", lambda: g.scalar.dma_start(T.first[:], T.res[:, 16:32]), [("res", 16, 32)], [])
+    return ops
+
+
+def _meet(a, b):
+    return a[0] == b[0] and (a[0] in PSUM or (a[1] < b[2] and b[1] < a[2]))
+
+
+def rank_program(g, core, T, topo):
+    rank = T.rank_of(core)
+    if rank is None:
+        return
+    ops = _plan(g, core, T, topo, rank)
+    n = len(ops)
+    deps = []
+    for j in range(n):
+        qj, kj, _, rj, wj = ops[j]
+        wj2 = wj + [r for r in rj if r[0] in PSUM]
+        need = {}
+        for i in range(j):
+            qi, ki, _, ri, wi = ops[i]
+            if qj is None or (qi == "t" and qj == "t") or ki == "r":
+                continue
+            wi2 = wi + [r for r in ri if r[0] in PSUM]
+            if any(_meet(a, b) for a in wi2 for b in rj + wj2) or any(_meet(a, b) for a in ri for b in wj2):
+                need[qi if ki == "c" else ("x", i)] = i
+        deps.append(need)
+    known, after, waits = {}, [None] * n, []
+    for j in range(n):
+        kn = known.setdefault(ops[j][0], {})
+        mine = []
+        for key, i in sorted(deps[j].items(), key=lambda t: -t[1]):
+            if kn.get(key, -1) >= i:
+                continue
+            mine.append(i)
+            for k2, v2 in after[i].items():
+                if kn.get(k2, -1) < v2:
+                    kn[k2] = v2
+        waits.append(mine)
+        mark = dict(kn) if ops[j][0] is not None else {}
+        mark[ops[j][0] if ops[j][1] == "c" else ("x", j)] = j
+        after[j] = mark
+    wanted = set(i for w in waits for i in w)
+    queue = {"v": g.vector, "s": g.scalar, "t": g.tensor, "g": g, "y": g.sync}
+    csem = {"v": "cv", "s": "cs", "t": "ct", "g": "cg"}
+    count, token, ndma = {}, {}, 0
+    for j in range(n):
+        q, kind, fn, _, _ = ops[j]
+        if q is None:
+            token[j] = (kind, N - 1)
+            count[kind] = N - 1
+            continue
+        for i in waits[j]:
+            queue[q].wait_ge(T.sem[token[i][0]], token[i][1])
+        ins = fn()
+        if kind == "d":
+            name = "d%d" % ndma
+            ndma += 1
+            ins.then_inc(T.sem[name], 16)
+            token[j] = (name, 16)
+            count[name] = 16
+        elif kind == "r":
+            count["sent"] = count.get("sent", 0) + N - 1
+        elif j in wanted:
+            count[csem[q]] = count.get(csem[q], 0) + 1
+            ins.then_inc(T.sem[csem[q]], 1)
+            token[j] = (csem[q], count[csem[q]])
+    for name, c in count.items():
+        g.wait_ge(T.sem[name], c)

@@ -6,35 +6,49 @@ M, N1, N2, N3 = 8192, 4096, 2048, 1024
 Q, QP = 2048, 256
 PAD = 16
 Z1, Z2, Z3, ZE = PAD, PAD + N1, PAD + N1 + N2, PAD + N1 + N2 + N3
+U1, U2, U3, UE = M + Z1, M + Z2, M + Z3, M + ZE
 L1, L2, L3, R1, R2, R3 = 0, 256, 384, 448, 704, 832
+ROUND = 201326592.0
+LIFT = 512
 CUT = {
-    "s_par": 1024,
-    "v_mid": 1280,
-    "lev1": (0, 1024, 2048, 3072, 3584, 4096),
-    "pe1": 512,
+    "p1": 1280, "p2": 3072,
+    "s_mid": 1024, "s_par": 2304,
+    "v_mid": 0,
+    "lev1": (("L", 0, 1024), ("R", 0, 1024), ("L", 1024, 2048), ("R", 1024, 2048), ("L", 2048, 3584),
+             ("R", 2048, 3072), ("R", 3072, 3584), ("T", 3584, 4096)),
+    "qa00": 256, "qa0": 1280, "qa1": 1280,
+    "c2": 1024,
     "v2": 1024,
-    "vo": 1024,
-    "qa0": 512,
-    "late": "copla",
-    "wl": 3584,
-    "vx": 1,
+    "v3": 512,
+    "vo": 1536,
+    "late": "eo1pn2ma",
+    "first": 3,
+    "s1": 1024,
+    "wl": (2560, 3584),
     "so": 1,
+    "vx": 0,
+    "clast": True,
+    "fin": (384, 896, 1408, 1792, 2048),
+    "ask": "late", "r1": True, "p0": 0, "fold": False, "width": 2, "caps": {1: (0, 1), 2: (2, 4)},
 }
+CUT.update({"p1": 2048, "p2": 3584, "so": 2})
 
 SCRATCH = {
-    "leafs": ("sbuf", [128, M + PAD], "bfloat16"),
+    "u": ("sbuf", [128, UE], "bfloat16"),
+    "x1": ("sbuf", [128, N1], "bfloat16"),
     "kid32": ("sbuf", [128, 896], "int32"),
     "kid": ("sbuf", [128, 896], "uint16"),
     "edg32": ("sbuf", [128, 128], "int32"),
     "cla32": ("sbuf", [128, 128], "int32"),
-    "ask32": ("sbuf", [128, 128], "int32"),
+    "gap32": ("sbuf", [128, 128], "int32"),
+    "col32": ("sbuf", [128, 128], "int32"),
+    "cla": ("sbuf", [128, 128], "uint16"),
+    "ask": ("sbuf", [128, 128], "uint16"),
     "eleaf": ("sbuf", [128, 128], "uint16"),
     "ebase": ("sbuf", [128, 128], "float32"),
     "wlist": ("sbuf", [128, 128], "uint16"),
     "slist": ("sbuf", [128, 128], "uint16"),
-    "aleaf": ("sbuf", [128, 128], "uint16"),
-    "ainner": ("sbuf", [128, 128], "uint16"),
-    "cnt": ("sbuf", [128, N2], "float32"),
+    "cnt": ("sbuf", [128, N1], "float32"),
     "par": ("sbuf", [128, M + PAD], "float32"),
     "sib2": ("sbuf", [128, N2], "float32"),
     "look": ("sbuf", [128, Q], "float32"),
@@ -42,31 +56,36 @@ SCRATCH = {
     "a2": ("sbuf", [128, N1], "bfloat16"),
     "a3": ("sbuf", [128, N2], "bfloat16"),
     "o2m": ("sbuf", [128, N2], "bfloat16"),
-    "zin": ("sbuf", [128, ZE], "bfloat16"),
     "zout": ("sbuf", [128, ZE], "bfloat16"),
-    "cl_s": ("sbuf", [128, Q], "bfloat16"),
-    "ci_s": ("sbuf", [128, Q], "bfloat16"),
-    "cl_r": ("sbuf", [128, Q], "bfloat16"),
-    "ci_r": ("sbuf", [128, Q], "bfloat16"),
+    "lift": ("sbuf", [128, LIFT], "bfloat16"),
+    "cap": ("sbuf", [128, QP], "bfloat16"),
+    "c_s": ("sbuf", [128, Q], "bfloat16"),
+    "c_r": ("sbuf", [128, Q], "bfloat16"),
+    "c_m": ("sbuf", [128, Q], "bfloat16"),
     "qa": ("sbuf", [128, Q], "bfloat16"),
     "qx": ("sbuf", [128, Q], "bfloat16"),
     "qo": ("sbuf", [128, Q], "bfloat16"),
     "mag": ("sbuf", [128, Q], "bfloat16"),
-    "ind": ("sbuf", [128, 8, 16, 16], "float16"),
-    "ones": ("sbuf", [128, 128], "float32"),
+    "ind": ("sbuf", [128, Q], "bfloat16"),
+    "ones": ("sbuf", [128, 8], "float32"),
+    "zero": ("sbuf", [128, 128], "float32"),
+    "zerob": ("sbuf", [128, 128], "bfloat16"),
     "idf": ("sbuf", [128, 128], "float32"),
     "id1": ("sbuf", [128, 128], "bfloat16"),
+    "id2": ("sbuf", [128, 128], "bfloat16"),
+    "idq": ("sbuf", [128, 128], "bfloat16"),
     "idm": ("sbuf", [128, 128], "bfloat16"),
+    "idn": ("sbuf", [128, 128], "bfloat16"),
+    "ids": ("sbuf", [128, 128], "bfloat16"),
     "sel": ("sbuf", [128, 16], "float32"),
     "bf": ("sbuf", [128, 144], "float32"),
-    "bh": ("sbuf", [128, 144], "float16"),
+    "bh": ("sbuf", [128, 144], "bfloat16"),
     "kt": ("sbuf", [128, 128], "bfloat16"),
-    "m48": ("sbuf", [128, 48], "float32"),
-    "n48": ("sbuf", [128, 48], "float32"),
-    "n16": ("sbuf", [128, 48], "float32"),
-    "key": ("sbuf", [128, 16], "int32"),
-    "res32": ("sbuf", [128, 32], "int32"),
-    "res": ("sbuf", [128, 32], "float32"),
+    "reset": ("sbuf", [128, 128], "float32"),
+    "key": ("sbuf", [128, 128], "float16"),
+    "low": ("sbuf", [128, 16], "float16"),
+    "resc": ("sbuf", [128, 128], "float32"),
+    "resf": ("sbuf", [128, 128], "float32"),
     "p0": ("psum", [128, 512], "float32"),
     "p1": ("psum", [128, 512], "float32"),
     "p2": ("psum", [128, 512], "float32"),
@@ -76,13 +95,14 @@ SCRATCH = {
     "pk": ("psum", [128, 512], "float32"),
     "pl": ("psum", [128, 512], "float32"),
 }
-NDMA = 18
-SEMAPHORES = ["cv", "cs", "ct", "cg", "sent", "got_ask", "got_cl", "got_ci"] + ["d%d" % i for i in range(NDMA)]
+NDMA = 24
+SEMAPHORES = ["cv", "cs", "ct", "cg", "sent", "got_ask", "got_c"] + ["d%d" % i for i in range(NDMA)]
 PSUM = ("p0", "p1", "p2", "p3", "ps", "pw", "pk", "pl")
 
 
 def _plan(g, core, T, topo, rank):
     ops = []
+    FINAL = list(zip((0,) + CUT["fin"][:-1], CUT["fin"], ("p0", "p1", "p2", "p3", "ps")))
 
     def add(q, kind, fn, rd, wr):
         ops.append((q, kind, fn, rd, wr))
@@ -95,6 +115,7 @@ def _plan(g, core, T, topo, rank):
 
     def ap(r): return T[r[0]][:, r[1]:r[2]]
     def ind(win, off): return ap(win).indirect(ap(off))
+    def full(name): return (name, 0, 128)
 
     def vfill(r, c): V(lambda: g.vector.memset(ap(r), c), [], [r])
     def vts(o, i, s1, s2, op0, op1=None):
@@ -109,41 +130,52 @@ def _plan(g, core, T, topo, rank):
         S(lambda: g.scalar.activation(ap(o), ind(win, off), f, bias=bias, scale=scale), [win, off], [o])
     def sput(win, off, src):
         S(lambda: g.scalar.activation(ind(win, off), ap(src), ACT.Silu), [off, src], [win])
-    def sact(o, i, f, bias=0.0): S(lambda: g.scalar.activation(ap(o), ap(i), f, bias=bias), [i], [o])
-    def mm(o, w, x, start, stop, xap=None):
-        P(lambda: g.tensor.matmul(ap(o), ap(w), ap(x) if xap is None else xap, start, stop), [w, x], [o])
+    def sact(o, i, f, bias=0.0, scale=1.0):
+        S(lambda: g.scalar.activation(ap(o), ap(i), f, bias=bias, scale=scale), [i], [o])
+    def mm(o, w, x, start, stop, xap=None, wap=None, oap=None):
+        P(lambda: g.tensor.matmul(ap(o) if oap is None else oap, ap(w) if wap is None else wap,
+                                  ap(x) if xap is None else xap, start, stop), [w, x], [o])
     def cols(base, a, b): return ("kid", base + a // 16, base + b // 16)
+    def part(name, a, b): return (name, a // 16, b // 16)
     def load(q, dst, src):
         D(q, lambda: (g.sync if q == "y" else g.scalar).dma_start(ap(dst), src), [], [dst])
-    def count_up(a, b):
-        G(lambda: g.iota(T.cnt[:, a:b], [[1, b - a]], PAD + a, 0, allow_small_or_imprecise_dtypes=True), [], [("cnt", a, b)])
+    def count(r, pattern, base):
+        G(lambda: g.iota(ap(r), pattern, base, 0, allow_small_or_imprecise_dtypes=True), [], [r])
+    def count_up(a, b): count(("cnt", a, b), [[1, b - a]], PAD + a)
+    def choose(o, i, pattern, op, fill, base, step):
+        G(lambda: g.affine_select(ap(o), ap(i), pattern, op, fill, base, step), [i], [o])
+    def dma_add(dst, src):
+        D("g", lambda: g.dma_start(ap(dst), ap(src), accum_op=ALU.add), [src, dst], [dst])
 
-    def send(src, dst, w, sem):
+    def send(src, dst, w, sem, steps, width, cap=None):
+        tos = [(rank + s) % N for s in steps]
         def fn():
             tr, used = [], []
-            for s in range(1, N):
-                q = (rank + s) % N
+            for q in tos:
                 to = T.cores[q]
-                e = [x for x in topo.engines(core, to) if x not in used][0]
-                used.append(e)
+                es = [x for x in topo.engines(core, to) if x not in used][:width]
+                used.extend(es)
                 rid, pid, _ = topo.addr(to)
-                tr.append(RemoteDMATransfer(dst_ids=[DstId(rid=rid, pnc=pid)], dma_engine_mask=1 << e, remote_sem=T.sem[sem],
-                                            src=T[src][:, q * w:(q + 1) * w], dst=T[dst][:, rank * w:(rank + 1) * w]))
+                a, b = T[src][:, q * w:(q + 1) * w], T[dst][:, rank * w:(rank + 1) * w]
+                way = dict(dst_ids=[DstId(rid=rid, pnc=pid)], dma_engine_mask=sum(1 << e for e in es), remote_sem=T.sem[sem])
+                if cap is None: tr.append(RemoteDMATransfer(src=a, dst=b, **way))
+                else: tr.append(RemoteDMATransfer(srcs=[a, T[cap][:]], dsts=[b], alu_op=3, **way))
             return g.remote_dma_fused(tr, local_sem=T.sem.sent)
-        others = [q for q in range(N) if q != rank]
-        add("g", "r", fn, [(src, q * w, (q + 1) * w) for q in others], [])
-        add(None, sem, None, [], [(dst, q * w, (q + 1) * w) for q in others])
+        add("g", ("r", width * len(tos)), fn, [(src, q * w, (q + 1) * w) for q in tos] + ([(cap, 0, w)] if cap else []), [])
+    def arrived(dst, w, sem, width):
+        add(None, (sem, width * (N - 1)), None, [], [(dst, q * w, (q + 1) * w) for q in range(N) if q != rank])
 
-    LEAF, PAR, ZIN, ZOUT = ("leafs", 0, M + PAD), ("par", 0, M + PAD), ("zin", 0, ZE), ("zout", 0, ZE)
+    LEAF, PAR, INNER, ZOUT, ALL = ("u", 0, M + PAD), ("par", 0, M + PAD), ("u", M, UE), ("zout", 0, ZE), ("u", 0, UE)
     PAR0, SIB = ("par", 0, M), ("sib2", 0, N2)
-    W1, W2 = ("zin", Z1, Z2), ("zin", Z2, Z3)
+    W1, W2, A3 = ("x1", 0, N1), ("u", U2, U3), ("a3", 0, N2)
 
-    def leaf(o, off): sget(o, LEAF, off, ACT.Abs, -4.5, 2.0)
-    def edge_leaf(a, b): sget(("qa", a, b), LEAF, ("eleaf", a // 16, b // 16), ACT.Abs, -2.25, 1.0)
+    def leaf(o, off): sget(o, LEAF, off, ACT.Abs, -2.25)
+    def edge_leaf(a, b):
+        if b > a: leaf(("qa", a, b), part("eleaf", a, b))
 
     def vpar(base, a, b):
         while a < b:
-            e = min(b, a + N2)
+            e = min(b, a + (512 if a < 512 else N2))
             off, src = cols(base, a, e), ("cnt", 0, e - a)
             V(lambda off=off, src=src, a=a: g.vector.tensor_scalar(ind(PAR0, off), ap(src), 1.0, float(a), ALU.mult, ALU.add), [off, src], [PAR0])
             a = e
@@ -151,190 +183,238 @@ def _plan(g, core, T, topo, rank):
     def to_list(pb, src, c0, c1, extra):
         o, x = (pb, c0, c1), (src, 16 * c0, 16 * c1)
         if extra is not None:
-            mm(o, ("idf", 0, 128), (extra, c0, c1), True, False)
+            mm(o, full("idf"), (extra, c0, c1), True, False)
         for s in range(16):
             mm(o, ("bf", 15 - s, 143 - s), x, s == 0 and extra is None, s == 15, xap=T[src][:, 16 * c0 + s:16 * c1:16])
 
-    def answer(name, lst, win, f, bias, scale, sem):
-        for a, b in ((0, rank), (rank + 1, N)):
-            if b > a:
-                sget((name + "_s", QP * a, QP * b), win, (lst, 16 * a, 16 * b), f, bias, scale)
-        send(name + "_s", name + "_r", QP, sem)
-        sget((name + "_r", QP * rank, QP * rank + QP), win, (lst, 16 * rank, 16 * rank + 16), f, bias, scale)
-
-    load("s", ("kid32", R3, 896), T.right[:, L3:R1])
+    def ask():
+        send("cla", "ask", 16, "got_ask", range(1, N), 1)
+        arrived("ask", 16, "got_ask", 1)
+    def columns():
+        vts(full("gap32"), full("cla32"), float(M), float(PAD), ALU.is_ge, ALU.mult)
+        vtt(full("col32"), full("cla32"), full("gap32"), ALU.add)
+        vcopy(full("cla"), full("col32"))
+        vcopy(("ask", 16 * rank, 16 * rank + 16), ("col32", 16 * rank, 16 * rank + 16))
+    early = CUT["ask"] == "early"
     load("y", ("kid32", L1, L2), T.left[:, L1:L2])
+    load("s", ("kid32", R3, 896), T.right[:, L3:R1])
     load("s", ("kid32", L3, R1), T.left[:, L3:R1])
-    load("y", ("kid32", R1, R2), T.right[:, L1:L2])
-    load("y", ("leafs", 0, M), T.leaf[:])
-    load("y", ("cla32", 0, 128), T.clade[:])
+    if CUT["r1"]: load("y", ("kid32", R1, R2), T.right[:, L1:L2])
+    if early: load("y", full("cla32"), T.clade[:])
+    load("y", ("u", 0, M), T.leaf[:])
+    if not CUT["r1"]: load("y", ("kid32", R1, R2), T.right[:, L1:L2])
+    load("y", full("edg32"), T.edge[:])
+    if not early: load("y", full("cla32"), T.clade[:])
     load("y", ("kid32", L2, L3), T.left[:, L2:L3])
     load("y", ("kid32", R2, R3), T.right[:, L2:L3])
-    load("y", ("edg32", 0, 128), T.edge[:])
-    vfill(("ones", 0, 128), 1.0)
+    vfill(("ones", 0, 8), 1.0)
+    vfill(full("zero"), 0.0)
+    vfill(full("zerob"), 0.0)
+    vfill(("u", M, U1), 3.0)
+    vfill(("u", U1, U2), 1.5)
     vfill(("bf", 0, 144), 0.0)
-    vfill(("leafs", M, M + PAD), 3.0)
-    vfill(("zin", 0, PAD), 3.0)
-    vfill(("zout", 0, PAD), 0.0)
-    vfill(("zout", Z3, ZE), 0.0)
-    vfill(("par", M, M + PAD), float(PAD - 1))
+    vfill(("bh", 0, 144), 0.0)
     count_up(0, 512)
     sact(("cnt", 512, 1024), ("cnt", 0, 512), ACT.Silu, 512.0)
-    G(lambda: g.affine_select(T.sel[:, 0:8], T.ones[:, 0:8], [[-16, 8]], ALU.is_ge, 0.0, 0, 1), [("ones", 0, 8)], [("sel", 0, 8)])
-    G(lambda: g.affine_select(T.sel[:, 8:16], T.sel[:, 0:8], [[16, 8]], ALU.is_ge, 0.0, 15, -1), [("sel", 0, 8)], [("sel", 8, 16)])
-    G(lambda: g.affine_select(T.idf[:], T.ones[:], [[-1, 128]], ALU.is_equal, 0.0, 0, 1), [("ones", 0, 128)], [("idf", 0, 128)])
+    choose(("sel", 0, 8), ("ones", 0, 8), [[-16, 8]], ALU.is_ge, 0.0, 0, 1)
+    choose(("sel", 8, 16), ("sel", 0, 8), [[16, 8]], ALU.is_ge, 0.0, 15, -1)
     count_up(1024, 2048)
-    G(lambda: g.iota(T.kt[:], [[1, 8], [0, 16]], 0, 0, allow_small_or_imprecise_dtypes=True), [], [("kt", 0, 128)])
+    for name, c in (("id1", 1.0), ("id2", 2.0), ("idq", 0.5), ("idm", -4.0), ("idn", -0.5), ("ids", 1.0 / 16)):
+        choose(full(name), full("zerob"), [[-1, 128]], ALU.not_equal, c, 0, 1)
+    choose(full("idf"), full("zero"), [[-1, 128]], ALU.not_equal, 1.0, 0, 1)
+    count(full("kt"), [[0, 16], [2, 8]], -7)
+    choose(full("reset"), full("zero"), [[0, 16], [1, 8]], ALU.not_equal, 1024.0, 0, 0)
+    def first_par():
+        vcopy(("kid", L1, L2), ("kid32", L1, L2))
+        vpar(L1, 0, CUT["p0"])
+    if CUT["p0"]: first_par()
     vts(("kid", R3, 896), ("kid32", R3, 896), float(-(M + N1)), None, ALU.add)
     vts(("kid", L3, R1), ("kid32", L3, R1), float(-(M + N1)), None, ALU.add)
-    vcopy(("kid", L1, L2), ("kid32", L1, L2))
+    if not CUT["p0"]: first_par()
     sput(SIB, cols(R3, 0, N3), ("cnt", 0, N3))
     sput(SIB, cols(L3, 0, N3), ("cnt", N3, N2))
-    vpar(L1, 0, 1024)
-    vcopy(("kid", R1, R2), ("kid32", R1, R2))
-    V(lambda: g.vector.tensor_scalar(T.bf[:, 15:143:16], T.sel[:, 8:16], 1.0 / 16, None, ALU.mult), [("sel", 8, 16)], [("bf", 0, 144)])
-    vcopy(("id1", 0, 128), ("idf", 0, 128))
-    vts(("idm", 0, 128), ("idf", 0, 128), -4.0, None, ALU.mult)
-    vcopy(("bh", 0, 144), ("bf", 0, 144))
-    vpar(L1, 1024, 2048)
-    send("cla32", "ask32", 16, "got_ask")
+    vpar(L1, CUT["p0"], 512)
+    for name in ("bf", "bh"):
+        V(lambda name=name: g.vector.tensor_scalar(T[name][:, 15:143:16], T.sel[:, 8:16], 1.0 / 16, None, ALU.mult), [("sel", 8, 16)], [(name, 0, 144)])
+    if CUT["r1"]: vcopy(("kid", R1, R2), ("kid32", R1, R2))
+    if early:
+        columns()
+        ask()
+    count(("zout", Z3, ZE), [[0, N3]], 0)
+    vpar(L1, 512, CUT["p1"])
+    if not CUT["r1"]: vcopy(("kid", R1, R2), ("kid32", R1, R2))
+    vpar(L1, CUT["p1"], CUT["p2"])
     to_list("ps", "sib2", 0, 128, None)
-    vpar(L1, 2048, 3072)
+    vts(full("eleaf"), full("edg32"), float(M), None, ALU.min)
+    vts(full("ebase"), full("edg32"), float(1 - M), 0.0, ALU.add, ALU.max)
+    if not early: columns()
     vts(("kid", L2, L3), ("kid32", L2, L3), float(-M), None, ALU.add)
     vts(("kid", R2, R3), ("kid32", R2, R3), float(-M), None, ALU.add)
-    vts(("eleaf", 0, 128), ("edg32", 0, 128), float(M), None, ALU.min)
-    vts(("ebase", 0, 128), ("edg32", 0, 128), float(1 - M), 0.0, ALU.add, ALU.max)
-    vcopy(("ask32", 16 * rank, 16 * rank + 16), ("cla32", 16 * rank, 16 * rank + 16))
-    vpar(L1, 3072, 4096)
-    vts(("aleaf", 0, 128), ("ask32", 0, 128), float(M), None, ALU.min)
-    vts(("ainner", 0, 128), ("ask32", 0, 128), float(PAD - M), 0.0, ALU.add, ALU.max)
-    vts(("slist", 0, 128), ("ps", 0, 128), 0.25 - PAD, None, ALU.add)
+    vfill(("zout", 0, PAD), 0.0)
+    vfill(("par", M, M + PAD), float(PAD - 1))
+    vfill(("cap", 0, QP), 2.5)
+    vfill(("lift", 0, LIFT), 1.5)
+    vpar(L1, CUT["p2"], N1)
+    vts(full("slist"), full("ps"), 0.25 - PAD, None, ALU.add)
     vpar(R1, CUT["s_par"] + CUT["v_mid"], N1)
 
-    cuts = CUT["lev1"]
-    for a, b in zip(cuts[:-1], cuts[1:]):
-        src, dst = ("a1", a, b), ("zin", Z1 + a, Z1 + b)
-        if a >= N1 - CUT["pe1"]:
+    for side, a, b in CUT["lev1"]:
+        src, dst = ("a1", a, b), ("x1", a, b)
+        if side == "L":
+            leaf(dst, cols(L1, a, b))
+        elif side == "R":
+            leaf(src, cols(R1, a, b))
+            dma_add(dst, src)
+        else:
             bank, left = ("pk" if b == N1 else "pl", 0, b - a), ("a1", N1 + a % 1024, N1 + a % 1024 + b - a)
             leaf(left, cols(L1, a, b))
             leaf(src, cols(R1, a, b))
-            mm(bank, ("id1", 0, 128), left, True, False)
-            mm(bank, ("id1", 0, 128), src, False, True)
-            vcopy(dst, bank)
-        else:
-            leaf(dst, cols(L1, a, b))
-            leaf(src, cols(R1, a, b))
-            D("g", lambda src=src, dst=dst: g.dma_start(ap(dst), ap(src), accum_op=ALU.add), [src, dst], [dst])
-    answer("cl", "aleaf", LEAF, ACT.Abs, -4.5, 2.0, "got_cl")
+            mm(bank, full("id1"), left, True, False)
+            mm(bank, full("id1"), src, False, True)
+            if b == N1:
+                edge_leaf(0, CUT["qa00"])
+            sact(dst, bank, ACT.Identity)
+    if not early: ask()
+    for a in (0, N2):
+        dma_add(("u", U1 + a, U1 + a + N2), ("x1", a, a + N2))
+    if CUT["s_par"] > N2:
+        count_up(N2, CUT["s_par"])
+    edge_leaf(CUT["qa00"], CUT["qa0"])
 
-    def gather(tab, n, h, lb, rb, win):
-        for base, o in ((lb, 0), (rb, n)):
-            if h:
-                vget2((tab, o, o + h), win, cols(base, 0, h), 2.0, 4.0, ALU.max, ALU.min)
-            sget((tab, o + h, o + n), win, cols(base, h, n), ACT.Sign, -3.0)
-    def sums(tab, n, banks, order):
-        for o in (0, n):
-            for b in order:
-                mm((banks[b], 0, 512), ("id1", 0, 128), (tab, o + 512 * b, o + 512 * b + 512), o == 0, o == n)
-    def evac(z, h, banks, order, on):
-        for b in order:
-            m = min(512, max(0, h - 512 * b))
-            for x, y, c in ((0, m, -3.0), (m, 512, 3.0)):
-                if y > x:
-                    dst = ("zin", z + 512 * b + x, z + 512 * b + y)
-                    if on[b] == "v": vts(dst, (banks[b], x, y), c, None, ALU.add)
-                    else: sact(dst, (banks[b], x, y), ACT.Identity, c)
-
-    v2, vo, qa0 = CUT["v2"], CUT["vo"], CUT["qa0"]
+    v2, v3, vo = CUT["v2"], CUT["v3"], CUT["vo"]
     ub = ["p0", "p1", "p2", "p3"]
-    gather("a2", N2, v2, L2, R2, W1)
-    if qa0:
-        edge_leaf(0, qa0)
-    sums("a2", N2, ub, (0, 2, 1, 3))
-    evac(Z2, v2, ub, (0, 2, 1, 3), "vvss")
+    order = sorted(range(4), key=lambda b: (512 * b if 512 * b < v2 else 512 * b - v2 + 1))
+    for b in order:
+        if 512 * b >= v2:
+            mm((ub[b], 0, 512), full("id2"), ("lift", 0, 512), True, False)
+    for base, o in ((L2, 0), (R2, N2)):
+        for a in range(0, v2, CUT["c2"]):
+            b = min(v2, a + CUT["c2"])
+            vget2(("a2", o + a, o + b), W1, cols(base, a, b), 1.0, 2.0, ALU.max, ALU.min)
+        for a in range(v2, N2, CUT["c2"]):
+            b = min(N2, a + CUT["c2"])
+            sget(("a2", o + a, o + b), W1, cols(base, a, b), ACT.Sign, -1.5)
+    edge_leaf(CUT["qa0"], CUT["qa1"])
+    if CUT["s_mid"]:
+        sput(PAR0, cols(R1, 0, CUT["s_mid"]), ("cnt", 0, CUT["s_mid"]))
+    for o in (0, N2):
+        for b in order:
+            mm((ub[b], 0, 512), full("id1" if 512 * b < v2 else "idq"), ("a2", o + 512 * b, o + 512 * b + 512), o == 0 and 512 * b < v2, o == N2)
+    for b in order:
+        vts(("u", U2 + 512 * b, U2 + 512 * b + 512), (ub[b], 0, 512), 2.5, 3.5, ALU.max, ALU.min)
     vpar(R1, CUT["s_par"], CUT["s_par"] + CUT["v_mid"])
-    gather("a3", N3, 0, L3, R3, W2)
-    sums("a3", N3, ["pk", "pl"], (0, 1))
-    A3 = ("a3", 0, N2)
-    vget(("zout", Z2, Z2 + vo), A3, ("slist", 0, vo // 16))
-    def term(b, w, name, start=False, stop=False):
-        mm((ub[b], 0, 512), (w, 0, 128), (name, 512 * b, 512 * b + 512), start, stop)
-    for b in range(4):
-        term(b, "idm", "cl_r", start=True)
-    for c in CUT["late"]:
-        if c == "c":
-            evac(Z3, 0, ["pk", "pl"], (0, 1), "ss")
-            answer("ci", "ainner", ZIN, ACT.Sign, -3.0, 1.0, "got_ci")
+
+    for base, o in ((L3, 0), (R3, N3)):
+        if v3: vget2(("a3", o, o + v3), W2, cols(base, 0, v3), 2.0, -6.0, ALU.mult, ALU.add)
+        if v3 < N3: sget(("a3", o + v3, o + N3), W2, cols(base, v3, N3), ACT.Identity, -6.0, 2.0)
+    for o in (0, N3):
+        for b, bank in enumerate(("pk", "pl")):
+            mm((bank, 0, 512), full("id1"), ("a3", o + 512 * b, o + 512 * b + 512), o == 0, o == N3)
+    vget(("zout", Z3 - vo, Z3), A3, part("slist", N2 - vo, N2))
+
+    def term(blk, w, name, start=False, stop=False):
+        mm((blk[2], 0, blk[1] - blk[0]), full(w), (name, blk[0], blk[1]), start, stop)
+    def wl(blk): return part("wlist", blk[0], blk[1])
+    def reg(name, blk): return (name, blk[0], blk[1])
+    nb = len(FINAL)
+    vx, so = CUT["vx"], CUT["so"]
+    own = ("c_s", QP * rank, QP * rank + QP)
+
+    def clades(qs):
+        sget(("c_s", QP * qs[0], QP * qs[-1] + QP), ALL, ("ask", 16 * qs[0], 16 * qs[-1] + 16), ACT.Abs, -4.5, 2.0)
+
+    def late(c):
+        if c == "e":
+            for b, bank in enumerate(("pk", "pl")):
+                sact(("u", U3 + 512 * b, U3 + 512 * b + 512), (bank, 0, 512), ACT.Identity, 3.0, 0.5)
         if c == "o":
-            for a in range(vo, N2, 512):
-                b = min(N2, a + 512)
-                sget(("zout", Z2 + a, Z2 + b), A3, ("slist", a // 16, b // 16), ACT.Identity)
-        if c == "p" and CUT["s_par"]:
-            sput(PAR0, cols(R1, 0, CUT["s_par"]), ("cnt", 0, CUT["s_par"]))
-        if c == "l":
-            for c0 in (0, 64):
-                sget(("look", 16 * c0, 16 * c0 + 1024), PAR, ("eleaf", c0, c0 + 64), ACT.Identity)
-                to_list("pw", "look", c0, c0 + 64, "ebase")
-        if c == "a" and qa0 < Q:
-            edge_leaf(qa0, Q)
+            for a in range(N2 - vo, 0, -512):
+                lo = max(0, a - 512)
+                sget(("zout", Z2 + lo, Z2 + a), A3, part("slist", lo, a), ACT.Identity)
+        if c in "12":
+            steps = range(1, 1 + CUT["first"]) if c == "1" else range(1 + CUT["first"], N)
+            qs = [(rank + s) % N for s in steps]
+            for run in ([q for q in qs if q > rank], [q for q in qs if q < rank]):
+                if run: clades(run)
+            send("c_s", "c_r", QP, "got_c", steps, CUT["width"], "cap" if CUT["fold"] else None)
+        if c == "2":
+            arrived("c_r", QP, "got_c", CUT["width"])
+            if CUT["fold"]: clades([rank])
+            else: sget(("c_r", own[1], own[2]), ALL, ("ask", 16 * rank, 16 * rank + 16), ACT.Abs, -4.5, 2.0)
+        if c == "p" and CUT["s_par"] > CUT["s_mid"]:
+            sput(PAR0, cols(R1, CUT["s_mid"], CUT["s_par"]), ("cnt", CUT["s_mid"], CUT["s_par"]))
+        if c in "nm":
+            c0, bank = (0, "pw") if c == "n" else (64, "pk")
+            sget(("look", 16 * c0, 16 * c0 + 1024), PAR, ("eleaf", c0, c0 + 64), ACT.Identity)
+            to_list(bank, "look", c0, c0 + 64, "ebase")
+        if c == "a":
+            edge_leaf(CUT["qa1"], Q)
+            for blk in FINAL:
+                term(blk, "id1", "qa", start=True)
+    for c in CUT["late"]:
+        late(c)
 
     O1 = ("zout", Z1, Z2)
     done = 0
-    pcut = sorted(set([0, min(vo, v2), v2, N2] + list(range(0, N2, 512))))
-    for a, b in zip(pcut[:-1], pcut[1:]):
+    pcut = sorted(set([0, v2, N2 - vo] + list(range(0, N2 + 1, CUT["s1"]))), reverse=True)
+    made = [False, False]
+    for b, a in zip(pcut[:-1], pcut[1:]):
         x = ("zout", Z2 + a, Z2 + b)
         if b <= v2:
-            vts(("o2m", a, b), x, -3.0, None, ALU.add)
+            vts(("o2m", a, b), x, 0.5, -1.5, ALU.mult, ALU.add)
             x = ("o2m", a, b)
         for base, o in ((L2, N2), (R2, 0)):
             off, y = cols(base, a, b), ("a2", o + a, o + b)
             V(lambda off=off, x=x, y=y: g.vector.tensor_tensor(ind(O1, off), ap(x), ap(y), ALU.add), [off, x, y], [O1])
-            if done < CUT["wl"] <= done + b - a:
-                vts(("wlist", 0, 128), ("pw", 0, 128), 0.25, None, ALU.add)
             done += b - a
+            for h, bank in enumerate(("pw", "pk")):
+                if not made[h] and done >= CUT["wl"][h]:
+                    made[h] = True
+                    vts(("wlist", 64 * h, 64 * h + 64), (bank, 64 * h, 64 * h + 64), 0.25, None, ALU.add)
+    cterm = "c_r" if CUT["fold"] else "c_m"
+    def cap(a, b):
+        if not CUT["fold"]: vts(("c_m", a, b), ("c_r", a, b), 2.5, None, ALU.min)
+    if CUT["fold"]: vts(("c_r", own[1], own[2]), own, 2.5, None, ALU.min)
+    if not CUT["clast"]: cap(0, Q)
 
-    def wl(b): return ("wlist", 32 * b, 32 * b + 32)
-    def blk(name, b): return (name, 512 * b, 512 * b + 512)
-    vx, so = CUT["vx"], CUT["so"]
-    for b in range(4):
-        term(b, "id1", "qa")
-    for b in range(4 - vx):
-        sget(blk("qx", b), ZIN, wl(b), ACT.Identity, -2.25, 0.75)
-        term(b, "id1", "qx")
-        term(b, "idm", "ci_r")
-    for b in range(4 - vx, 4):
-        term(b, "idm", "ci_r")
-    for b in range(so):
-        sget(blk("qo", b), ZOUT, wl(b), ACT.Sign)
-    for b in range(so, 4):
-        vget2(blk("qo", b), ZOUT, wl(b), -1.0, 1.0, ALU.max, ALU.min)
-        if b >= 4 - vx:
-            vget2(blk("qx", b), ZIN, wl(b), 0.75, -2.25, ALU.mult, ALU.add)
-    for b in range(4):
-        if b >= 4 - vx:
-            term(b, "id1", "qx")
-        term(b, "id1", "qo", stop=True)
-    for b in range(4):
-        sact(blk("mag", b), (ub[b], 0, 512), ACT.Abs, 5.25)
-    for pb, k0, k1 in (("pk", 0, 6), ("pl", 6, 8)):
-        for b in range(k0 // 2, k1 // 2):
-            V(lambda b=b: g.vector.tensor_scalar(T.ind[:, 2 * b:2 * b + 2, :, :], T.mag[:, 512 * b:512 * b + 512], 4.625, 128.0, ALU.is_ge, ALU.mult),
-              [blk("mag", b)], [blk("ind", b)])
-        o = (pb, 0, 16 * (k1 - k0))
-        mm(o, ("id1", 0, 128), ("kt", 16 * k0, 16 * k1), True, False)
-        for h in range(16):
-            mm(o, ("bh", 15 - h, 143 - h), ("ind", QP * k0, QP * k1), False, h == 15, xap=T.ind[:, k0:k1, h, :])
-    vcopy(("m48", 0, 48), ("pk", 0, 48))
-    vtt(("n48", 0, 48), ("pk", 48, 96), ("m48", 0, 48), ALU.min)
-    vtt(("n16", 0, 16), ("n48", 0, 16), ("n48", 16, 32), ALU.min)
-    vtt(("n16", 16, 32), ("pl", 0, 16), ("n48", 32, 48), ALU.min)
-    vtt(("n16", 32, 48), ("pl", 16, 32), ("n16", 0, 16), ALU.min)
-    vtt(("key", 0, 16), ("n16", 16, 32), ("n16", 32, 48), ALU.min)
-    vts(("res32", 0, 16), ("key", 0, 16), 3, None, ALU.arith_shift_right)
-    vts(("res32", 16, 32), ("key", 0, 16), 7, None, ALU.bitwise_and)
-    vcopy(("res", 0, 32), ("res32", 0, 32))
-    D("y", lambda: g.sync.dma_start(T.cost[:], T.res[:, 0:16]), [("res", 0, 16)], [])
-    D("s", lambda: g.scalar.dma_start(T.first[:], T.res[:, 16:32]), [("res", 16, 32)], [])
+    for blk in FINAL[:nb - vx]:
+        sget(reg("qx", blk), INNER, wl(blk), ACT.Identity, -4.5, 1.5)
+        term(blk, "id1", "qx")
+    if not CUT["clast"]:
+        for blk in FINAL:
+            term(blk, "idm", cterm)
+    mm(full("pl"), full("id1"), full("kt"), True, False)
+    for blk in FINAL[:so]:
+        sget(reg("qo", blk), ZOUT, wl(blk), ACT.Sign)
+    for b, blk in enumerate(FINAL):
+        if b >= so:
+            vget2(reg("qo", blk), ZOUT, wl(blk), -0.5, 0.5, ALU.max, ALU.min)
+        if b >= nb - vx:
+            vget2(reg("qx", blk), INNER, wl(blk), 1.5, -4.5, ALU.mult, ALU.add)
+        if CUT["clast"] and b in CUT["caps"]:
+            cap(FINAL[CUT["caps"][b][0]][0], FINAL[CUT["caps"][b][1]][1])
+    for b, blk in enumerate(FINAL):
+        if b >= nb - vx:
+            term(blk, "id1", "qx")
+        term(blk, "id1" if b < so else "id2", "qo", stop=not CUT["clast"])
+        if CUT["clast"]:
+            term(blk, "idm", cterm, stop=True)
+    for blk in FINAL:
+        sact(reg("mag", blk), (blk[2], 0, blk[1] - blk[0]), ACT.Abs, 5.25)
+    for blk in FINAL:
+        vts(reg("ind", blk), reg("mag", blk), 4.625, 256.0, ALU.is_ge, ALU.mult)
+        for a in range(blk[0], blk[1], 128):
+            s = 8 * (a // 128 % 2) + a // QP
+            mm(full("pl"), ("ind", a, a + 128), ("bh", 15 - s, 143 - s), False, a == Q - 128)
+    V(lambda: g.vector.tensor_tensor_scan(T.key[:], T.reset[:], T.pl[:, 0:128], 0.0, ALU.add, ALU.min), [full("reset"), full("pl")], [full("key")])
+    V(lambda: g.vector.tensor_scalar(T.low[:], T.key[:, 7:128:8], ROUND, -ROUND, ALU.add, ALU.add), [full("key")], [("low", 0, 16)])
+    mm(full("pw"), full("key"), full("idq"), True, False, wap=T.key[:, 7:128:8], oap=T.pw[0:16, 0:128])
+    mm(full("pk"), ("low", 0, 16), full("ids"), True, True, oap=T.pk[0:16, 0:128])
+    mm(full("pw"), ("low", 0, 16), full("idn"), False, True, oap=T.pw[0:16, 0:128])
+    S(lambda: g.scalar.activation(T.resc[0:16, :], T.pk[0:16, 0:128], ACT.Identity), [full("pk")], [full("resc")])
+    V(lambda: g.vector.tensor_scalar(T.resf[0:16, :], T.pw[0:16, 0:128], 3.5, None, ALU.add), [full("pw")], [full("resf")])
+    D("s", lambda: g.scalar.dma_start(T.cost[:], T.resc[0:16, :]), [full("resc")], [])
+    D("y", lambda: g.sync.dma_start(T.first[:], T.resf[0:16, :]), [full("resf")], [])
     return ops
 
 
@@ -355,7 +435,7 @@ def rank_program(g, core, T, topo):
         need = {}
         for i in range(j):
             qi, ki, _, ri, wi = ops[i]
-            if qj is None or (qi == "t" and qj == "t") or ki == "r":
+            if qj is None or (qi == "t" and qj == "t") or (qi == "g" and ki[0] == "r"):
                 continue
             wi2 = wi + [r for r in ri if r[0] in PSUM]
             if any(_meet(a, b) for a in wi2 for b in rj + wj2) or any(_meet(a, b) for a in ri for b in wj2):
@@ -383,8 +463,8 @@ def rank_program(g, core, T, topo):
     for j in range(n):
         q, kind, fn, _, _ = ops[j]
         if q is None:
-            token[j] = (kind, N - 1)
-            count[kind] = N - 1
+            token[j] = kind
+            count[kind[0]] = kind[1]
             continue
         for i in waits[j]:
             queue[q].wait_ge(T.sem[token[i][0]], token[i][1])
@@ -395,8 +475,8 @@ def rank_program(g, core, T, topo):
             ins.then_inc(T.sem[name], 16)
             token[j] = (name, 16)
             count[name] = 16
-        elif kind == "r":
-            count["sent"] = count.get("sent", 0) + N - 1
+        elif kind[0] == "r":
+            count["sent"] = count.get("sent", 0) + kind[1]
         elif j in wanted:
             count[csem[q]] = count.get(csem[q], 0) + 1
             ins.then_inc(T.sem[csem[q]], 1)

@@ -7,31 +7,25 @@ Q, QP = 2048, 256
 PAD = 16
 Z1, Z2, Z3, ZE = PAD, PAD + N1, PAD + N1 + N2, PAD + N1 + N2 + N3
 U1, U2, U3, UE = M + Z1, M + Z2, M + Z3, M + ZE
-L1, L2, L3, R1, R2, R3 = 0, 256, 384, 448, 704, 832
+L1, R1, L3, R3, L2, R2 = 0, 256, 512, 576, 640, 768
 ROUND = 201326592.0
-LIFT = 512
+V2 = 1024
 CUT = {
-    "p1": 1280, "p2": 3072,
-    "s_mid": 1024, "s_par": 2304,
-    "v_mid": 0,
-    "lev1": (("L", 0, 1024), ("R", 0, 1024), ("L", 1024, 2048), ("R", 1024, 2048), ("L", 2048, 3584),
-             ("R", 2048, 3072), ("R", 3072, 3584), ("T", 3584, 4096)),
-    "qa00": 256, "qa0": 1280, "qa1": 1280,
-    "c2": 1024,
-    "v2": 1024,
+    "p0": 256, "p1": 2304, "p2": 3072,
+    "s_par": (1152, 2048, 3328),
+    "lev1": (0, 864, 1600, 2400, 3072),
+    "lefts": (0, 1600, 3072),
+    "qa00": 640, "qa0": 1024,
     "v3": 512,
-    "vo": 1536,
-    "late": "eo1pn2ma",
+    "late": "p1dqn2zma3",
     "first": 3,
-    "s1": 1024,
-    "wl": (2560, 3584),
-    "so": 1,
+    "wl": (3072, 3584),
     "vx": 0,
-    "clast": True,
-    "fin": (384, 896, 1408, 1792, 2048),
-    "ask": "late", "r1": True, "p0": 0, "fold": False, "width": 2, "caps": {1: (0, 1), 2: (2, 4)},
+    "so": 2,
+    "caps": {0: (0, 2), 3: (3, 4)},
+    "fin": (512, 896, 1408, 1792, 2048),
+    "ford": (0, 1, 2, 3, 4),
 }
-CUT.update({"p1": 2048, "p2": 3584, "so": 2})
 
 SCRATCH = {
     "u": ("sbuf", [128, UE], "bfloat16"),
@@ -42,8 +36,8 @@ SCRATCH = {
     "cla32": ("sbuf", [128, 128], "int32"),
     "gap32": ("sbuf", [128, 128], "int32"),
     "col32": ("sbuf", [128, 128], "int32"),
-    "cla": ("sbuf", [128, 128], "uint16"),
     "ask": ("sbuf", [128, 128], "uint16"),
+    "asked": ("sbuf", [128, 128], "uint16"),
     "eleaf": ("sbuf", [128, 128], "uint16"),
     "ebase": ("sbuf", [128, 128], "float32"),
     "wlist": ("sbuf", [128, 128], "uint16"),
@@ -52,13 +46,13 @@ SCRATCH = {
     "par": ("sbuf", [128, M + PAD], "float32"),
     "sib2": ("sbuf", [128, N2], "float32"),
     "look": ("sbuf", [128, Q], "float32"),
-    "a1": ("sbuf", [128, N1 + 1024], "bfloat16"),
+    "a1": ("sbuf", [128, N1], "bfloat16"),
+    "raw": ("sbuf", [128, 1024], "bfloat16"),
+    "big": ("sbuf", [128, 1024], "bfloat16"),
     "a2": ("sbuf", [128, N1], "bfloat16"),
     "a3": ("sbuf", [128, N2], "bfloat16"),
     "o2m": ("sbuf", [128, N2], "bfloat16"),
     "zout": ("sbuf", [128, ZE], "bfloat16"),
-    "lift": ("sbuf", [128, LIFT], "bfloat16"),
-    "cap": ("sbuf", [128, QP], "bfloat16"),
     "c_s": ("sbuf", [128, Q], "bfloat16"),
     "c_r": ("sbuf", [128, Q], "bfloat16"),
     "c_m": ("sbuf", [128, Q], "bfloat16"),
@@ -67,7 +61,7 @@ SCRATCH = {
     "qo": ("sbuf", [128, Q], "bfloat16"),
     "mag": ("sbuf", [128, Q], "bfloat16"),
     "ind": ("sbuf", [128, Q], "bfloat16"),
-    "ones": ("sbuf", [128, 8], "float32"),
+    "ones": ("sbuf", [128, PAD], "float32"),
     "zero": ("sbuf", [128, 128], "float32"),
     "zerob": ("sbuf", [128, 128], "bfloat16"),
     "idf": ("sbuf", [128, 128], "float32"),
@@ -147,7 +141,7 @@ def _plan(g, core, T, topo, rank):
     def dma_add(dst, src):
         D("g", lambda: g.dma_start(ap(dst), ap(src), accum_op=ALU.add), [src, dst], [dst])
 
-    def send(src, dst, w, sem, steps, width, cap=None):
+    def send(src, dst, w, sem, steps, width, here, there):
         tos = [(rank + s) % N for s in steps]
         def fn():
             tr, used = [], []
@@ -156,18 +150,16 @@ def _plan(g, core, T, topo, rank):
                 es = [x for x in topo.engines(core, to) if x not in used][:width]
                 used.extend(es)
                 rid, pid, _ = topo.addr(to)
-                a, b = T[src][:, q * w:(q + 1) * w], T[dst][:, rank * w:(rank + 1) * w]
-                way = dict(dst_ids=[DstId(rid=rid, pnc=pid)], dma_engine_mask=sum(1 << e for e in es), remote_sem=T.sem[sem])
-                if cap is None: tr.append(RemoteDMATransfer(src=a, dst=b, **way))
-                else: tr.append(RemoteDMATransfer(srcs=[a, T[cap][:]], dsts=[b], alu_op=3, **way))
+                tr.append(RemoteDMATransfer(dst_ids=[DstId(rid=rid, pnc=pid)], dma_engine_mask=sum(1 << e for e in es), remote_sem=T.sem[sem],
+                                            src=T[src][:, here(q) * w:(here(q) + 1) * w], dst=T[dst][:, there(q) * w:(there(q) + 1) * w]))
             return g.remote_dma_fused(tr, local_sem=T.sem.sent)
-        add("g", ("r", width * len(tos)), fn, [(src, q * w, (q + 1) * w) for q in tos] + ([(cap, 0, w)] if cap else []), [])
-    def arrived(dst, w, sem, width):
-        add(None, (sem, width * (N - 1)), None, [], [(dst, q * w, (q + 1) * w) for q in range(N) if q != rank])
+        add("g", ("r", width * len(tos)), fn, [(src, here(q) * w, (here(q) + 1) * w) for q in tos], [])
+    def arrived(dst, w, sem, width, kept):
+        add(None, (sem, width * (N - 1)), None, [], [(dst, q * w, (q + 1) * w) for q in range(N) if q != kept])
 
     LEAF, PAR, INNER, ZOUT, ALL = ("u", 0, M + PAD), ("par", 0, M + PAD), ("u", M, UE), ("zout", 0, ZE), ("u", 0, UE)
     PAR0, SIB = ("par", 0, M), ("sib2", 0, N2)
-    W1, W2, A3 = ("x1", 0, N1), ("u", U2, U3), ("a3", 0, N2)
+    W1, W2, W3 = ("x1", 0, N1), ("u", U2, U3), ("u", U3, UE)
 
     def leaf(o, off): sget(o, LEAF, off, ACT.Abs, -2.25)
     def edge_leaf(a, b):
@@ -175,7 +167,7 @@ def _plan(g, core, T, topo, rank):
 
     def vpar(base, a, b):
         while a < b:
-            e = min(b, a + (512 if a < 512 else N2))
+            e = min(b, a + N2)
             off, src = cols(base, a, e), ("cnt", 0, e - a)
             V(lambda off=off, src=src, a=a: g.vector.tensor_scalar(ind(PAR0, off), ap(src), 1.0, float(a), ALU.mult, ALU.add), [off, src], [PAR0])
             a = e
@@ -187,168 +179,137 @@ def _plan(g, core, T, topo, rank):
         for s in range(16):
             mm(o, ("bf", 15 - s, 143 - s), x, s == 0 and extra is None, s == 15, xap=T[src][:, 16 * c0 + s:16 * c1:16])
 
-    def ask():
-        send("cla", "ask", 16, "got_ask", range(1, N), 1)
-        arrived("ask", 16, "got_ask", 1)
-    def columns():
-        vts(full("gap32"), full("cla32"), float(M), float(PAD), ALU.is_ge, ALU.mult)
-        vtt(full("col32"), full("cla32"), full("gap32"), ALU.add)
-        vcopy(full("cla"), full("col32"))
-        vcopy(("ask", 16 * rank, 16 * rank + 16), ("col32", 16 * rank, 16 * rank + 16))
-    early = CUT["ask"] == "early"
-    load("y", ("kid32", L1, L2), T.left[:, L1:L2])
-    load("s", ("kid32", R3, 896), T.right[:, L3:R1])
-    load("s", ("kid32", L3, R1), T.left[:, L3:R1])
-    if CUT["r1"]: load("y", ("kid32", R1, R2), T.right[:, L1:L2])
-    if early: load("y", full("cla32"), T.clade[:])
+    load("y", ("kid32", L1, R1), T.left[:, 0:256])
+    load("s", ("kid32", R3, L2), T.right[:, 384:448])
+    load("s", ("kid32", L3, R3), T.left[:, 384:448])
+    load("y", ("kid32", R1, L3), T.right[:, 0:256])
     load("y", ("u", 0, M), T.leaf[:])
-    if not CUT["r1"]: load("y", ("kid32", R1, R2), T.right[:, L1:L2])
     load("y", full("edg32"), T.edge[:])
-    if not early: load("y", full("cla32"), T.clade[:])
-    load("y", ("kid32", L2, L3), T.left[:, L2:L3])
-    load("y", ("kid32", R2, R3), T.right[:, L2:L3])
-    vfill(("ones", 0, 8), 1.0)
+    load("y", full("cla32"), T.clade[:])
+    load("y", ("kid32", L2, R2), T.left[:, 256:384])
+    load("y", ("kid32", R2, 896), T.right[:, 256:384])
+    vfill(("ones", 0, PAD), 1.0)
     vfill(full("zero"), 0.0)
     vfill(full("zerob"), 0.0)
-    vfill(("u", M, U1), 3.0)
-    vfill(("u", U1, U2), 1.5)
     vfill(("bf", 0, 144), 0.0)
     vfill(("bh", 0, 144), 0.0)
-    count_up(0, 512)
-    sact(("cnt", 512, 1024), ("cnt", 0, 512), ACT.Silu, 512.0)
+    vfill(("u", U1, U1 + 512), 1.5)
+    sact(("par", M, M + PAD), ("ones", 0, PAD), ACT.Silu, PAD - 2.0)
+    count_up(0, 256)
+    for a in (256, 512):
+        vts(("cnt", a, 2 * a), ("cnt", 0, a), float(a), None, ALU.add)
+    count_up(1024, 2048)
     choose(("sel", 0, 8), ("ones", 0, 8), [[-16, 8]], ALU.is_ge, 0.0, 0, 1)
     choose(("sel", 8, 16), ("sel", 0, 8), [[16, 8]], ALU.is_ge, 0.0, 15, -1)
-    count_up(1024, 2048)
+    count(("u", M, U1), [[0, PAD]], 3)
     for name, c in (("id1", 1.0), ("id2", 2.0), ("idq", 0.5), ("idm", -4.0), ("idn", -0.5), ("ids", 1.0 / 16)):
         choose(full(name), full("zerob"), [[-1, 128]], ALU.not_equal, c, 0, 1)
     choose(full("idf"), full("zero"), [[-1, 128]], ALU.not_equal, 1.0, 0, 1)
-    count(full("kt"), [[0, 16], [2, 8]], -7)
-    choose(full("reset"), full("zero"), [[0, 16], [1, 8]], ALU.not_equal, 1024.0, 0, 0)
-    def first_par():
-        vcopy(("kid", L1, L2), ("kid32", L1, L2))
-        vpar(L1, 0, CUT["p0"])
-    if CUT["p0"]: first_par()
-    vts(("kid", R3, 896), ("kid32", R3, 896), float(-(M + N1)), None, ALU.add)
-    vts(("kid", L3, R1), ("kid32", L3, R1), float(-(M + N1)), None, ALU.add)
-    if not CUT["p0"]: first_par()
+    for a in (512, 1024, 2048):
+        D("y", lambda a=a: g.sync.dma_start(T.u[:, U1 + a:U1 + 2 * a], T.u[:, U1:U1 + a]), [("u", U1, U1 + a)], [("u", U1 + a, U1 + 2 * a)])
+    vts(("kid", R3, L2), ("kid32", R3, L2), float(-(M + N1)), None, ALU.add)
+    vcopy(("kid", L1, R1), ("kid32", L1, R1))
     sput(SIB, cols(R3, 0, N3), ("cnt", 0, N3))
-    sput(SIB, cols(L3, 0, N3), ("cnt", N3, N2))
-    vpar(L1, CUT["p0"], 512)
+    vpar(L1, 0, CUT["p0"])
+    vts(("kid", L3, R3), ("kid32", L3, R3), float(-(M + N1)), None, ALU.add)
+    sput(SIB, cols(L3, 0, N3), ("cnt", 0, N3))
+    vcopy(("kid", R1, L3), ("kid32", R1, L3))
+    vpar(L1, CUT["p0"], CUT["p1"])
     for name in ("bf", "bh"):
         V(lambda name=name: g.vector.tensor_scalar(T[name][:, 15:143:16], T.sel[:, 8:16], 1.0 / 16, None, ALU.mult), [("sel", 8, 16)], [(name, 0, 144)])
-    if CUT["r1"]: vcopy(("kid", R1, R2), ("kid32", R1, R2))
-    if early:
-        columns()
-        ask()
-    count(("zout", Z3, ZE), [[0, N3]], 0)
-    vpar(L1, 512, CUT["p1"])
-    if not CUT["r1"]: vcopy(("kid", R1, R2), ("kid32", R1, R2))
-    vpar(L1, CUT["p1"], CUT["p2"])
     to_list("ps", "sib2", 0, 128, None)
+    vts(full("gap32"), full("cla32"), float(M), float(PAD), ALU.is_ge, ALU.mult)
     vts(full("eleaf"), full("edg32"), float(M), None, ALU.min)
+    vtt(full("col32"), full("cla32"), full("gap32"), ALU.add)
     vts(full("ebase"), full("edg32"), float(1 - M), 0.0, ALU.add, ALU.max)
-    if not early: columns()
-    vts(("kid", L2, L3), ("kid32", L2, L3), float(-M), None, ALU.add)
-    vts(("kid", R2, R3), ("kid32", R2, R3), float(-M), None, ALU.add)
-    vfill(("zout", 0, PAD), 0.0)
-    vfill(("par", M, M + PAD), float(PAD - 1))
-    vfill(("cap", 0, QP), 2.5)
-    vfill(("lift", 0, LIFT), 1.5)
+    vcopy(full("ask"), full("col32"))
+    vts(("kid", L2, 896), ("kid32", L2, 896), float(-M), None, ALU.add)
+    top = CUT["lev1"][-1]
+    vget(("raw", 0, N1 - top), LEAF, cols(R1, top, N1))
+    vpar(L1, CUT["p1"], CUT["p2"])
+    vts(("big", 0, N1 - top), ("raw", 0, N1 - top), 2.0, -3.0, ALU.is_ge, ALU.mult)
     vpar(L1, CUT["p2"], N1)
     vts(full("slist"), full("ps"), 0.25 - PAD, None, ALU.add)
-    vpar(R1, CUT["s_par"] + CUT["v_mid"], N1)
+    vpar(R1, CUT["s_par"][-1], N1)
+    v3 = CUT["v3"]
+    ub = ["p0", "p1", "p2", "p3"]
+    for b in (2, 3):
+        mm((ub[b], 0, 512), full("id2"), ("u", U1, U1 + 512), True, False)
 
-    for side, a, b in CUT["lev1"]:
-        src, dst = ("a1", a, b), ("x1", a, b)
-        if side == "L":
-            leaf(dst, cols(L1, a, b))
-        elif side == "R":
-            leaf(src, cols(R1, a, b))
-            dma_add(dst, src)
-        else:
-            bank, left = ("pk" if b == N1 else "pl", 0, b - a), ("a1", N1 + a % 1024, N1 + a % 1024 + b - a)
-            leaf(left, cols(L1, a, b))
-            leaf(src, cols(R1, a, b))
-            mm(bank, full("id1"), left, True, False)
-            mm(bank, full("id1"), src, False, True)
-            if b == N1:
-                edge_leaf(0, CUT["qa00"])
-            sact(dst, bank, ACT.Identity)
-    if not early: ask()
+    ends, lefts = CUT["lev1"], dict(zip(CUT["lefts"][:-1], CUT["lefts"][1:]))
+    for a, b in zip(ends[:-1], ends[1:]):
+        if a in lefts: leaf(("x1", a, lefts[a]), cols(L1, a, lefts[a]))
+        leaf(("a1", a, b), cols(R1, a, b))
+        dma_add(("x1", a, b), ("a1", a, b))
+    leaf(("a1", top, N1), cols(L1, top, N1))
+    tb = (("pk", top, top + 512), ("pl", top + 512, N1))
+    for bank, a, b in tb:
+        for i, name in enumerate(("raw", "big")):
+            mm((bank, 0, b - a), full("idq"), (name, a - top, b - top), i == 0, False)
+        mm((bank, 0, b - a), full("id1"), ("a1", a, b), False, True)
+    edge_leaf(0, CUT["qa00"])
+    for bank, a, b in tb:
+        sact(("x1", a, b), (bank, 0, b - a), ACT.Identity, 0.75)
+    send("ask", "asked", 16, "got_ask", range(1, N), 1, lambda q: q, lambda q: (rank - q) % N)
+    arrived("asked", 16, "got_ask", 1, 0)
     for a in (0, N2):
         dma_add(("u", U1 + a, U1 + a + N2), ("x1", a, a + N2))
-    if CUT["s_par"] > N2:
-        count_up(N2, CUT["s_par"])
+    count_up(N2, CUT["s_par"][-1])
+    choose(("o2m", 0, V2), ("x1", 0, V2), [[0, V2]], ALU.is_gt, -1.5, 0, 0)
     edge_leaf(CUT["qa00"], CUT["qa0"])
 
-    v2, v3, vo = CUT["v2"], CUT["v3"], CUT["vo"]
-    ub = ["p0", "p1", "p2", "p3"]
-    order = sorted(range(4), key=lambda b: (512 * b if 512 * b < v2 else 512 * b - v2 + 1))
-    for b in order:
-        if 512 * b >= v2:
-            mm((ub[b], 0, 512), full("id2"), ("lift", 0, 512), True, False)
+    order = (0, 2, 1, 3)
     for base, o in ((L2, 0), (R2, N2)):
-        for a in range(0, v2, CUT["c2"]):
-            b = min(v2, a + CUT["c2"])
-            vget2(("a2", o + a, o + b), W1, cols(base, a, b), 1.0, 2.0, ALU.max, ALU.min)
-        for a in range(v2, N2, CUT["c2"]):
-            b = min(N2, a + CUT["c2"])
-            sget(("a2", o + a, o + b), W1, cols(base, a, b), ACT.Sign, -1.5)
-    edge_leaf(CUT["qa0"], CUT["qa1"])
-    if CUT["s_mid"]:
-        sput(PAR0, cols(R1, 0, CUT["s_mid"]), ("cnt", 0, CUT["s_mid"]))
+        vget2(("a2", o, o + V2), W1, cols(base, 0, V2), 1.0, 2.0, ALU.max, ALU.min)
+        sget(("a2", o + V2, o + N2), W1, cols(base, V2, N2), ACT.Sign, -1.5)
+    sput(PAR0, cols(R1, 0, CUT["s_par"][0]), ("cnt", 0, CUT["s_par"][0]))
     for o in (0, N2):
         for b in order:
-            mm((ub[b], 0, 512), full("id1" if 512 * b < v2 else "idq"), ("a2", o + 512 * b, o + 512 * b + 512), o == 0 and 512 * b < v2, o == N2)
+            mm((ub[b], 0, 512), full("id1" if b < 2 else "idq"), ("a2", o + 512 * b, o + 512 * b + 512), o == 0 and b < 2, o == N2)
     for b in order:
         vts(("u", U2 + 512 * b, U2 + 512 * b + 512), (ub[b], 0, 512), 2.5, 3.5, ALU.max, ALU.min)
-    vpar(R1, CUT["s_par"], CUT["s_par"] + CUT["v_mid"])
 
-    for base, o in ((L3, 0), (R3, N3)):
-        if v3: vget2(("a3", o, o + v3), W2, cols(base, 0, v3), 2.0, -6.0, ALU.mult, ALU.add)
-        if v3 < N3: sget(("a3", o + v3, o + N3), W2, cols(base, v3, N3), ACT.Identity, -6.0, 2.0)
-    for o in (0, N3):
-        for b, bank in enumerate(("pk", "pl")):
-            mm((bank, 0, 512), full("id1"), ("a3", o + 512 * b, o + 512 * b + 512), o == 0, o == N3)
-    vget(("zout", Z3 - vo, Z3), A3, part("slist", N2 - vo, N2))
+    def vjoin(o, win, off, y, op):
+        V(lambda: g.vector.tensor_tensor(ap(o), ind(win, off), ap(y), op), [win, off, y], [o])
+    sget(("a3", v3, N3), W2, cols(L3, v3, N3), ACT.Identity, -3.0)
+    vget2(("a3", 0, v3), W2, cols(L3, 0, v3), -3.0, 1.0, ALU.add, ALU.mult)
+    for a, b in ((0, v3), (v3, N3)):
+        vjoin(("u", U3 + a, U3 + b), W2, cols(R3, a, b), ("a3", a, b), ALU.add)
+    for a, b in ((V2, N2), (0, V2)):
+        vjoin(("zout", Z2 + a, Z2 + b), W3, part("slist", a, b), ("u", U2 + a, U2 + b), ALU.subtract)
+    vts(("o2m", V2, N2), ("zout", Z2 + V2, Z3), 2.0, None, ALU.mult)
 
     def term(blk, w, name, start=False, stop=False):
         mm((blk[2], 0, blk[1] - blk[0]), full(w), (name, blk[0], blk[1]), start, stop)
     def wl(blk): return part("wlist", blk[0], blk[1])
     def reg(name, blk): return (name, blk[0], blk[1])
-    nb = len(FINAL)
-    vx, so = CUT["vx"], CUT["so"]
-    own = ("c_s", QP * rank, QP * rank + QP)
-
-    def clades(qs):
-        sget(("c_s", QP * qs[0], QP * qs[-1] + QP), ALL, ("ask", 16 * qs[0], 16 * qs[-1] + 16), ACT.Abs, -4.5, 2.0)
+    def clades(o, off): sget(o, ALL, off, ACT.Abs, -4.5, 2.0)
 
     def late(c):
-        if c == "e":
-            for b, bank in enumerate(("pk", "pl")):
-                sact(("u", U3 + 512 * b, U3 + 512 * b + 512), (bank, 0, 512), ACT.Identity, 3.0, 0.5)
-        if c == "o":
-            for a in range(N2 - vo, 0, -512):
-                lo = max(0, a - 512)
-                sget(("zout", Z2 + lo, Z2 + a), A3, part("slist", lo, a), ACT.Identity)
+        if c == "d":
+            dma_add(("o2m", 0, V2), ("zout", Z2, Z2 + V2))
+        if c == "z":
+            count(("zout", 0, PAD), [[0, PAD]], 0)
+            count(("zout", Z3, ZE), [[0, N3]], 0)
+            count(full("kt"), [[0, 16], [2, 8]], -7)
+            choose(full("reset"), full("zero"), [[0, 16], [1, 8]], ALU.not_equal, 1024.0, 0, 0)
         if c in "12":
-            steps = range(1, 1 + CUT["first"]) if c == "1" else range(1 + CUT["first"], N)
-            qs = [(rank + s) % N for s in steps]
-            for run in ([q for q in qs if q > rank], [q for q in qs if q < rank]):
-                if run: clades(run)
-            send("c_s", "c_r", QP, "got_c", steps, CUT["width"], "cap" if CUT["fold"] else None)
+            a, b = (1, 1 + CUT["first"]) if c == "1" else (1 + CUT["first"], N)
+            clades(("c_s", QP * a, QP * b), ("asked", 16 * a, 16 * b))
+            send("c_s", "c_r", QP, "got_c", range(a, b), 2, lambda q: (q - rank) % N, lambda q: rank)
         if c == "2":
-            arrived("c_r", QP, "got_c", CUT["width"])
-            if CUT["fold"]: clades([rank])
-            else: sget(("c_r", own[1], own[2]), ALL, ("ask", 16 * rank, 16 * rank + 16), ACT.Abs, -4.5, 2.0)
-        if c == "p" and CUT["s_par"] > CUT["s_mid"]:
-            sput(PAR0, cols(R1, CUT["s_mid"], CUT["s_par"]), ("cnt", CUT["s_mid"], CUT["s_par"]))
+            arrived("c_r", QP, "got_c", 2, rank)
+        if c == "3":
+            clades(("c_r", QP * rank, QP * rank + QP), ("ask", 16 * rank, 16 * rank + 16))
+        if c in "pq":
+            a, b = CUT["s_par"][:2] if c == "p" else CUT["s_par"][1:]
+            sput(PAR0, cols(R1, a, b), ("cnt", a, b))
         if c in "nm":
             c0, bank = (0, "pw") if c == "n" else (64, "pk")
             sget(("look", 16 * c0, 16 * c0 + 1024), PAR, ("eleaf", c0, c0 + 64), ACT.Identity)
             to_list(bank, "look", c0, c0 + 64, "ebase")
         if c == "a":
-            edge_leaf(CUT["qa1"], Q)
+            edge_leaf(CUT["qa0"], Q)
             for blk in FINAL:
                 term(blk, "id1", "qa", start=True)
     for c in CUT["late"]:
@@ -356,56 +317,45 @@ def _plan(g, core, T, topo, rank):
 
     O1 = ("zout", Z1, Z2)
     done = 0
-    pcut = sorted(set([0, v2, N2 - vo] + list(range(0, N2 + 1, CUT["s1"]))), reverse=True)
-    made = [False, False]
-    for b, a in zip(pcut[:-1], pcut[1:]):
-        x = ("zout", Z2 + a, Z2 + b)
-        if b <= v2:
-            vts(("o2m", a, b), x, 0.5, -1.5, ALU.mult, ALU.add)
-            x = ("o2m", a, b)
+    for lo in (V2, 0):
         for base, o in ((L2, N2), (R2, 0)):
-            off, y = cols(base, a, b), ("a2", o + a, o + b)
-            V(lambda off=off, x=x, y=y: g.vector.tensor_tensor(ind(O1, off), ap(x), ap(y), ALU.add), [off, x, y], [O1])
-            done += b - a
-            for h, bank in enumerate(("pw", "pk")):
-                if not made[h] and done >= CUT["wl"][h]:
-                    made[h] = True
-                    vts(("wlist", 64 * h, 64 * h + 64), (bank, 64 * h, 64 * h + 64), 0.25, None, ALU.add)
-    cterm = "c_r" if CUT["fold"] else "c_m"
-    def cap(a, b):
-        if not CUT["fold"]: vts(("c_m", a, b), ("c_r", a, b), 2.5, None, ALU.min)
-    if CUT["fold"]: vts(("c_r", own[1], own[2]), own, 2.5, None, ALU.min)
-    if not CUT["clast"]: cap(0, Q)
+            stops = sorted(set([done, done + V2] + [w for w in CUT["wl"] if done < w < done + V2]))
+            for x, y in zip(stops[:-1], stops[1:]):
+                a, b = lo + x - done, lo + y - done
+                off, up, sib = cols(base, a, b), ("o2m", a, b), ("a2", o + a, o + b)
+                V(lambda off=off, up=up, sib=sib: g.vector.tensor_tensor(ind(O1, off), ap(up), ap(sib), ALU.add), [off, up, sib], [O1])
+                for h, bank in enumerate(("pw", "pk")):
+                    if CUT["wl"][h] == y:
+                        vts(("wlist", 64 * h, 64 * h + 64), (bank, 64 * h, 64 * h + 64), 0.25, None, ALU.add)
+            done += V2
 
-    for blk in FINAL[:nb - vx]:
-        sget(reg("qx", blk), INNER, wl(blk), ACT.Identity, -4.5, 1.5)
+    so = CUT["so"]
+    vx = CUT["vx"]
+    for a, b in ((0, Q // 2), (Q // 2, Q - vx)):
+        sget(("qx", a, b), INNER, part("wlist", a, b), ACT.Identity, -4.5, 1.5)
+    if vx: vget2(("qx", Q - vx, Q), INNER, part("wlist", Q - vx, Q), 1.5, -4.5, ALU.mult, ALU.add)
+    for blk in FINAL:
         term(blk, "id1", "qx")
-    if not CUT["clast"]:
-        for blk in FINAL:
-            term(blk, "idm", cterm)
     mm(full("pl"), full("id1"), full("kt"), True, False)
     for blk in FINAL[:so]:
         sget(reg("qo", blk), ZOUT, wl(blk), ACT.Sign)
     for b, blk in enumerate(FINAL):
         if b >= so:
             vget2(reg("qo", blk), ZOUT, wl(blk), -0.5, 0.5, ALU.max, ALU.min)
-        if b >= nb - vx:
-            vget2(reg("qx", blk), INNER, wl(blk), 1.5, -4.5, ALU.mult, ALU.add)
-        if CUT["clast"] and b in CUT["caps"]:
-            cap(FINAL[CUT["caps"][b][0]][0], FINAL[CUT["caps"][b][1]][1])
-    for b, blk in enumerate(FINAL):
-        if b >= nb - vx:
-            term(blk, "id1", "qx")
-        term(blk, "id1" if b < so else "id2", "qo", stop=not CUT["clast"])
-        if CUT["clast"]:
-            term(blk, "idm", cterm, stop=True)
+        if b in CUT["caps"]:
+            x, y = FINAL[CUT["caps"][b][0]][0], FINAL[CUT["caps"][b][1]][1]
+            vts(("c_m", x, y), ("c_r", x, y), 2.5, None, ALU.min)
+    for b in CUT["ford"]:
+        term(FINAL[b], "id1" if b < so else "id2", "qo")
+        term(FINAL[b], "idm", "c_m", stop=True)
+    FINAL = [FINAL[b] for b in CUT["ford"]]
     for blk in FINAL:
         sact(reg("mag", blk), (blk[2], 0, blk[1] - blk[0]), ACT.Abs, 5.25)
     for blk in FINAL:
         vts(reg("ind", blk), reg("mag", blk), 4.625, 256.0, ALU.is_ge, ALU.mult)
         for a in range(blk[0], blk[1], 128):
             s = 8 * (a // 128 % 2) + a // QP
-            mm(full("pl"), ("ind", a, a + 128), ("bh", 15 - s, 143 - s), False, a == Q - 128)
+            mm(full("pl"), ("ind", a, a + 128), ("bh", 15 - s, 143 - s), False, a == FINAL[-1][1] - 128)
     V(lambda: g.vector.tensor_tensor_scan(T.key[:], T.reset[:], T.pl[:, 0:128], 0.0, ALU.add, ALU.min), [full("reset"), full("pl")], [full("key")])
     V(lambda: g.vector.tensor_scalar(T.low[:], T.key[:, 7:128:8], ROUND, -ROUND, ALU.add, ALU.add), [full("key")], [("low", 0, 16)])
     mm(full("pw"), full("key"), full("idq"), True, False, wap=T.key[:, 7:128:8], oap=T.pw[0:16, 0:128])

from concourse.bass import DstId, RemoteDMATransfer
from concourse.mybir import AluOpType as ALU, ActivationFunctionType as ACT

N = 8
M, N1, N2, N3 = 8192, 4096, 2048, 1024
Q, QP = 2048, 256
PAD = 16
Z1, Z2, Z3, ZE = PAD, PAD + N1, PAD + N1 + N2, PAD + N1 + N2 + N3
U1, U2, U3, UE = M + Z1, M + Z2, M + Z3, M + ZE
L1, R1, L3, R3, L2, R2 = 0, 256, 512, 576, 640, 768
ROUND = 201326592.0
V2 = 1024
CUT = {
    "p0": 256, "p1": 2304, "p2": 3072,
    "s_par": (1152, 2048, 3328),
    "lev1": (0, 864, 1600, 2400, 3072),
    "lefts": (0, 1600, 3072),
    "qa00": 640, "qa0": 1024,
    "v3": 512,
    "late": "p1dqn2zma3",
    "first": 3,
    "wl": (3072, 3584),
    "vx": 0,
    "so": 2,
    "caps": {0: (0, 2), 3: (3, 4)},
    "fin": (512, 896, 1408, 1792, 2048),
    "ford": (0, 1, 2, 3, 4),
}

SCRATCH = {
    "u": ("sbuf", [128, UE], "bfloat16"),
    "x1": ("sbuf", [128, N1], "bfloat16"),
    "kid32": ("sbuf", [128, 896], "int32"),
    "kid": ("sbuf", [128, 896], "uint16"),
    "edg32": ("sbuf", [128, 128], "int32"),
    "cla32": ("sbuf", [128, 128], "int32"),
    "gap32": ("sbuf", [128, 128], "int32"),
    "col32": ("sbuf", [128, 128], "int32"),
    "ask": ("sbuf", [128, 128], "uint16"),
    "asked": ("sbuf", [128, 128], "uint16"),
    "eleaf": ("sbuf", [128, 128], "uint16"),
    "ebase": ("sbuf", [128, 128], "float32"),
    "wlist": ("sbuf", [128, 128], "uint16"),
    "slist": ("sbuf", [128, 128], "uint16"),
    "cnt": ("sbuf", [128, N1], "float32"),
    "par": ("sbuf", [128, M + PAD], "float32"),
    "sib2": ("sbuf", [128, N2], "float32"),
    "look": ("sbuf", [128, Q], "float32"),
    "a1": ("sbuf", [128, N1], "bfloat16"),
    "raw": ("sbuf", [128, 1024], "bfloat16"),
    "big": ("sbuf", [128, 1024], "bfloat16"),
    "a2": ("sbuf", [128, N1], "bfloat16"),
    "a3": ("sbuf", [128, N2], "bfloat16"),
    "o2m": ("sbuf", [128, N2], "bfloat16"),
    "zout": ("sbuf", [128, ZE], "bfloat16"),
    "c_s": ("sbuf", [128, Q], "bfloat16"),
    "c_r": ("sbuf", [128, Q], "bfloat16"),
    "c_m": ("sbuf", [128, Q], "bfloat16"),
    "qa": ("sbuf", [128, Q], "bfloat16"),
    "qx": ("sbuf", [128, Q], "bfloat16"),
    "qo": ("sbuf", [128, Q], "bfloat16"),
    "mag": ("sbuf", [128, Q], "bfloat16"),
    "ind": ("sbuf", [128, Q], "bfloat16"),
    "ones": ("sbuf", [128, PAD], "float32"),
    "zero": ("sbuf", [128, 128], "float32"),
    "zerob": ("sbuf", [128, 128], "bfloat16"),
    "idf": ("sbuf", [128, 128], "float32"),
    "id1": ("sbuf", [128, 128], "bfloat16"),
    "id2": ("sbuf", [128, 128], "bfloat16"),
    "idq": ("sbuf", [128, 128], "bfloat16"),
    "idm": ("sbuf", [128, 128], "bfloat16"),
    "idn": ("sbuf", [128, 128], "bfloat16"),
    "ids": ("sbuf", [128, 128], "bfloat16"),
    "sel": ("sbuf", [128, 16], "float32"),
    "bf": ("sbuf", [128, 144], "float32"),
    "bh": ("sbuf", [128, 144], "bfloat16"),
    "kt": ("sbuf", [128, 128], "bfloat16"),
    "reset": ("sbuf", [128, 128], "float32"),
    "key": ("sbuf", [128, 128], "float16"),
    "low": ("sbuf", [128, 16], "float16"),
    "resc": ("sbuf", [128, 128], "float32"),
    "resf": ("sbuf", [128, 128], "float32"),
    "p0": ("psum", [128, 512], "float32"),
    "p1": ("psum", [128, 512], "float32"),
    "p2": ("psum", [128, 512], "float32"),
    "p3": ("psum", [128, 512], "float32"),
    "ps": ("psum", [128, 512], "float32"),
    "pw": ("psum", [128, 512], "float32"),
    "pk": ("psum", [128, 512], "float32"),
    "pl": ("psum", [128, 512], "float32"),
}
NDMA = 24
SEMAPHORES = ["cv", "cs", "ct", "cg", "sent", "got_ask", "got_c"] + ["d%d" % i for i in range(NDMA)]
PSUM = ("p0", "p1", "p2", "p3", "ps", "pw", "pk", "pl")


def _plan(g, core, T, topo, rank):
    ops = []
    FINAL = list(zip((0,) + CUT["fin"][:-1], CUT["fin"], ("p0", "p1", "p2", "p3", "ps")))

    def add(q, kind, fn, rd, wr):
        ops.append((q, kind, fn, rd, wr))

    def V(fn, rd, wr): add("v", "c", fn, rd, wr)
    def S(fn, rd, wr): add("s", "c", fn, rd, wr)
    def G(fn, rd, wr): add("g", "c", fn, rd, wr)
    def P(fn, rd, wr): add("t", "c", fn, rd, wr)
    def D(q, fn, rd, wr): add(q, "d", fn, rd, wr)

    def ap(r): return T[r[0]][:, r[1]:r[2]]
    def ind(win, off): return ap(win).indirect(ap(off))
    def full(name): return (name, 0, 128)

    def vfill(r, c): V(lambda: g.vector.memset(ap(r), c), [], [r])
    def vts(o, i, s1, s2, op0, op1=None):
        if op1 is None: V(lambda: g.vector.tensor_scalar(ap(o), ap(i), s1, None, op0), [i], [o])
        else: V(lambda: g.vector.tensor_scalar(ap(o), ap(i), s1, s2, op0, op1), [i], [o])
    def vcopy(o, i): V(lambda: g.vector.tensor_copy(ap(o), ap(i)), [i], [o])
    def vtt(o, a, b, op): V(lambda: g.vector.tensor_tensor(ap(o), ap(a), ap(b), op), [a, b], [o])
    def vget2(o, win, off, s1, s2, op0, op1):
        V(lambda: g.vector.tensor_scalar(ap(o), ind(win, off), s1, s2, op0, op1), [win, off], [o])
    def vget(o, win, off): V(lambda: g.vector.tensor_copy(ap(o), ind(win, off)), [win, off], [o])
    def sget(o, win, off, f, bias=0.0, scale=1.0):
        S(lambda: g.scalar.activation(ap(o), ind(win, off), f, bias=bias, scale=scale), [win, off], [o])
    def sput(win, off, src):
        S(lambda: g.scalar.activation(ind(win, off), ap(src), ACT.Silu), [off, src], [win])
    def sact(o, i, f, bias=0.0, scale=1.0):
        S(lambda: g.scalar.activation(ap(o), ap(i), f, bias=bias, scale=scale), [i], [o])
    def mm(o, w, x, start, stop, xap=None, wap=None, oap=None):
        P(lambda: g.tensor.matmul(ap(o) if oap is None else oap, ap(w) if wap is None else wap,
                                  ap(x) if xap is None else xap, start, stop), [w, x], [o])
    def cols(base, a, b): return ("kid", base + a // 16, base + b // 16)
    def part(name, a, b): return (name, a // 16, b // 16)
    def load(q, dst, src):
        D(q, lambda: (g.sync if q == "y" else g.scalar).dma_start(ap(dst), src), [], [dst])
    def count(r, pattern, base):
        G(lambda: g.iota(ap(r), pattern, base, 0, allow_small_or_imprecise_dtypes=True), [], [r])
    def count_up(a, b): count(("cnt", a, b), [[1, b - a]], PAD + a)
    def choose(o, i, pattern, op, fill, base, step):
        G(lambda: g.affine_select(ap(o), ap(i), pattern, op, fill, base, step), [i], [o])
    def dma_add(dst, src):
        D("g", lambda: g.dma_start(ap(dst), ap(src), accum_op=ALU.add), [src, dst], [dst])

    def send(src, dst, w, sem, steps, width, here, there):
        tos = [(rank + s) % N for s in steps]
        def fn():
            tr, used = [], []
            for q in tos:
                to = T.cores[q]
                es = [x for x in topo.engines(core, to) if x not in used][:width]
                used.extend(es)
                rid, pid, _ = topo.addr(to)
                tr.append(RemoteDMATransfer(dst_ids=[DstId(rid=rid, pnc=pid)], dma_engine_mask=sum(1 << e for e in es), remote_sem=T.sem[sem],
                                            src=T[src][:, here(q) * w:(here(q) + 1) * w], dst=T[dst][:, there(q) * w:(there(q) + 1) * w]))
            return g.remote_dma_fused(tr, local_sem=T.sem.sent)
        add("g", ("r", width * len(tos)), fn, [(src, here(q) * w, (here(q) + 1) * w) for q in tos], [])
    def arrived(dst, w, sem, width, kept):
        add(None, (sem, width * (N - 1)), None, [], [(dst, q * w, (q + 1) * w) for q in range(N) if q != kept])

    LEAF, PAR, INNER, ZOUT, ALL = ("u", 0, M + PAD), ("par", 0, M + PAD), ("u", M, UE), ("zout", 0, ZE), ("u", 0, UE)
    PAR0, SIB = ("par", 0, M), ("sib2", 0, N2)
    W1, W2, W3 = ("x1", 0, N1), ("u", U2, U3), ("u", U3, UE)

    def leaf(o, off): sget(o, LEAF, off, ACT.Abs, -2.25)
    def edge_leaf(a, b):
        if b > a: leaf(("qa", a, b), part("eleaf", a, b))

    def vpar(base, a, b):
        while a < b:
            e = min(b, a + N2)
            off, src = cols(base, a, e), ("cnt", 0, e - a)
            V(lambda off=off, src=src, a=a: g.vector.tensor_scalar(ind(PAR0, off), ap(src), 1.0, float(a), ALU.mult, ALU.add), [off, src], [PAR0])
            a = e

    def to_list(pb, src, c0, c1, extra):
        o, x = (pb, c0, c1), (src, 16 * c0, 16 * c1)
        if extra is not None:
            mm(o, full("idf"), (extra, c0, c1), True, False)
        for s in range(16):
            mm(o, ("bf", 15 - s, 143 - s), x, s == 0 and extra is None, s == 15, xap=T[src][:, 16 * c0 + s:16 * c1:16])

    load("y", ("kid32", L1, R1), T.left[:, 0:256])
    load("s", ("kid32", R3, L2), T.right[:, 384:448])
    load("s", ("kid32", L3, R3), T.left[:, 384:448])
    load("y", ("kid32", R1, L3), T.right[:, 0:256])
    load("y", ("u", 0, M), T.leaf[:])
    load("y", full("edg32"), T.edge[:])
    load("y", full("cla32"), T.clade[:])
    load("y", ("kid32", L2, R2), T.left[:, 256:384])
    load("y", ("kid32", R2, 896), T.right[:, 256:384])
    vfill(("ones", 0, PAD), 1.0)
    vfill(full("zero"), 0.0)
    vfill(full("zerob"), 0.0)
    vfill(("bf", 0, 144), 0.0)
    vfill(("bh", 0, 144), 0.0)
    vfill(("u", U1, U1 + 512), 1.5)
    sact(("par", M, M + PAD), ("ones", 0, PAD), ACT.Silu, PAD - 2.0)
    count_up(0, 256)
    for a in (256, 512):
        vts(("cnt", a, 2 * a), ("cnt", 0, a), float(a), None, ALU.add)
    count_up(1024, 2048)
    choose(("sel", 0, 8), ("ones", 0, 8), [[-16, 8]], ALU.is_ge, 0.0, 0, 1)
    choose(("sel", 8, 16), ("sel", 0, 8), [[16, 8]], ALU.is_ge, 0.0, 15, -1)
    count(("u", M, U1), [[0, PAD]], 3)
    for name, c in (("id1", 1.0), ("id2", 2.0), ("idq", 0.5), ("idm", -4.0), ("idn", -0.5), ("ids", 1.0 / 16)):
        choose(full(name), full("zerob"), [[-1, 128]], ALU.not_equal, c, 0, 1)
    choose(full("idf"), full("zero"), [[-1, 128]], ALU.not_equal, 1.0, 0, 1)
    for a in (512, 1024, 2048):
        D("y", lambda a=a: g.sync.dma_start(T.u[:, U1 + a:U1 + 2 * a], T.u[:, U1:U1 + a]), [("u", U1, U1 + a)], [("u", U1 + a, U1 + 2 * a)])
    vts(("kid", R3, L2), ("kid32", R3, L2), float(-(M + N1)), None, ALU.add)
    vcopy(("kid", L1, R1), ("kid32", L1, R1))
    sput(SIB, cols(R3, 0, N3), ("cnt", 0, N3))
    vpar(L1, 0, CUT["p0"])
    vts(("kid", L3, R3), ("kid32", L3, R3), float(-(M + N1)), None, ALU.add)
    sput(SIB, cols(L3, 0, N3), ("cnt", 0, N3))
    vcopy(("kid", R1, L3), ("kid32", R1, L3))
    vpar(L1, CUT["p0"], CUT["p1"])
    for name in ("bf", "bh"):
        V(lambda name=name: g.vector.tensor_scalar(T[name][:, 15:143:16], T.sel[:, 8:16], 1.0 / 16, None, ALU.mult), [("sel", 8, 16)], [(name, 0, 144)])
    to_list("ps", "sib2", 0, 128, None)
    vts(full("gap32"), full("cla32"), float(M), float(PAD), ALU.is_ge, ALU.mult)
    vts(full("eleaf"), full("edg32"), float(M), None, ALU.min)
    vtt(full("col32"), full("cla32"), full("gap32"), ALU.add)
    vts(full("ebase"), full("edg32"), float(1 - M), 0.0, ALU.add, ALU.max)
    vcopy(full("ask"), full("col32"))
    vts(("kid", L2, 896), ("kid32", L2, 896), float(-M), None, ALU.add)
    top = CUT["lev1"][-1]
    vget(("raw", 0, N1 - top), LEAF, cols(R1, top, N1))
    vpar(L1, CUT["p1"], CUT["p2"])
    vts(("big", 0, N1 - top), ("raw", 0, N1 - top), 2.0, -3.0, ALU.is_ge, ALU.mult)
    vpar(L1, CUT["p2"], N1)
    vts(full("slist"), full("ps"), 0.25 - PAD, None, ALU.add)
    vpar(R1, CUT["s_par"][-1], N1)
    v3 = CUT["v3"]
    ub = ["p0", "p1", "p2", "p3"]
    for b in (2, 3):
        mm((ub[b], 0, 512), full("id2"), ("u", U1, U1 + 512), True, False)

    ends, lefts = CUT["lev1"], dict(zip(CUT["lefts"][:-1], CUT["lefts"][1:]))
    for a, b in zip(ends[:-1], ends[1:]):
        if a in lefts: leaf(("x1", a, lefts[a]), cols(L1, a, lefts[a]))
        leaf(("a1", a, b), cols(R1, a, b))
        dma_add(("x1", a, b), ("a1", a, b))
    leaf(("a1", top, N1), cols(L1, top, N1))
    tb = (("pk", top, top + 512), ("pl", top + 512, N1))
    for bank, a, b in tb:
        for i, name in enumerate(("raw", "big")):
            mm((bank, 0, b - a), full("idq"), (name, a - top, b - top), i == 0, False)
        mm((bank, 0, b - a), full("id1"), ("a1", a, b), False, True)
    edge_leaf(0, CUT["qa00"])
    for bank, a, b in tb:
        sact(("x1", a, b), (bank, 0, b - a), ACT.Identity, 0.75)
    send("ask", "asked", 16, "got_ask", range(1, N), 1, lambda q: q, lambda q: (rank - q) % N)
    arrived("asked", 16, "got_ask", 1, 0)
    for a in (0, N2):
        dma_add(("u", U1 + a, U1 + a + N2), ("x1", a, a + N2))
    count_up(N2, CUT["s_par"][-1])
    choose(("o2m", 0, V2), ("x1", 0, V2), [[0, V2]], ALU.is_gt, -1.5, 0, 0)
    edge_leaf(CUT["qa00"], CUT["qa0"])

    order = (0, 2, 1, 3)
    for base, o in ((L2, 0), (R2, N2)):
        vget2(("a2", o, o + V2), W1, cols(base, 0, V2), 1.0, 2.0, ALU.max, ALU.min)
        sget(("a2", o + V2, o + N2), W1, cols(base, V2, N2), ACT.Sign, -1.5)
    sput(PAR0, cols(R1, 0, CUT["s_par"][0]), ("cnt", 0, CUT["s_par"][0]))
    for o in (0, N2):
        for b in order:
            mm((ub[b], 0, 512), full("id1" if b < 2 else "idq"), ("a2", o + 512 * b, o + 512 * b + 512), o == 0 and b < 2, o == N2)
    for b in order:
        vts(("u", U2 + 512 * b, U2 + 512 * b + 512), (ub[b], 0, 512), 2.5, 3.5, ALU.max, ALU.min)

    def vjoin(o, win, off, y, op):
        V(lambda: g.vector.tensor_tensor(ap(o), ind(win, off), ap(y), op), [win, off, y], [o])
    sget(("a3", v3, N3), W2, cols(L3, v3, N3), ACT.Identity, -3.0)
    vget2(("a3", 0, v3), W2, cols(L3, 0, v3), -3.0, 1.0, ALU.add, ALU.mult)
    for a, b in ((0, v3), (v3, N3)):
        vjoin(("u", U3 + a, U3 + b), W2, cols(R3, a, b), ("a3", a, b), ALU.add)
    for a, b in ((V2, N2), (0, V2)):
        vjoin(("zout", Z2 + a, Z2 + b), W3, part("slist", a, b), ("u", U2 + a, U2 + b), ALU.subtract)
    vts(("o2m", V2, N2), ("zout", Z2 + V2, Z3), 2.0, None, ALU.mult)

    def term(blk, w, name, start=False, stop=False):
        mm((blk[2], 0, blk[1] - blk[0]), full(w), (name, blk[0], blk[1]), start, stop)
    def wl(blk): return part("wlist", blk[0], blk[1])
    def reg(name, blk): return (name, blk[0], blk[1])
    def clades(o, off): sget(o, ALL, off, ACT.Abs, -4.5, 2.0)

    def late(c):
        if c == "d":
            dma_add(("o2m", 0, V2), ("zout", Z2, Z2 + V2))
        if c == "z":
            count(("zout", 0, PAD), [[0, PAD]], 0)
            count(("zout", Z3, ZE), [[0, N3]], 0)
            count(full("kt"), [[0, 16], [2, 8]], -7)
            choose(full("reset"), full("zero"), [[0, 16], [1, 8]], ALU.not_equal, 1024.0, 0, 0)
        if c in "12":
            a, b = (1, 1 + CUT["first"]) if c == "1" else (1 + CUT["first"], N)
            clades(("c_s", QP * a, QP * b), ("asked", 16 * a, 16 * b))
            send("c_s", "c_r", QP, "got_c", range(a, b), 2, lambda q: (q - rank) % N, lambda q: rank)
        if c == "2":
            arrived("c_r", QP, "got_c", 2, rank)
        if c == "3":
            clades(("c_r", QP * rank, QP * rank + QP), ("ask", 16 * rank, 16 * rank + 16))
        if c in "pq":
            a, b = CUT["s_par"][:2] if c == "p" else CUT["s_par"][1:]
            sput(PAR0, cols(R1, a, b), ("cnt", a, b))
        if c in "nm":
            c0, bank = (0, "pw") if c == "n" else (64, "pk")
            sget(("look", 16 * c0, 16 * c0 + 1024), PAR, ("eleaf", c0, c0 + 64), ACT.Identity)
            to_list(bank, "look", c0, c0 + 64, "ebase")
        if c == "a":
            edge_leaf(CUT["qa0"], Q)
            for blk in FINAL:
                term(blk, "id1", "qa", start=True)
    for c in CUT["late"]:
        late(c)

    O1 = ("zout", Z1, Z2)
    done = 0
    for lo in (V2, 0):
        for base, o in ((L2, N2), (R2, 0)):
            stops = sorted(set([done, done + V2] + [w for w in CUT["wl"] if done < w < done + V2]))
            for x, y in zip(stops[:-1], stops[1:]):
                a, b = lo + x - done, lo + y - done
                off, up, sib = cols(base, a, b), ("o2m", a, b), ("a2", o + a, o + b)
                V(lambda off=off, up=up, sib=sib: g.vector.tensor_tensor(ind(O1, off), ap(up), ap(sib), ALU.add), [off, up, sib], [O1])
                for h, bank in enumerate(("pw", "pk")):
                    if CUT["wl"][h] == y:
                        vts(("wlist", 64 * h, 64 * h + 64), (bank, 64 * h, 64 * h + 64), 0.25, None, ALU.add)
            done += V2

    so = CUT["so"]
    vx = CUT["vx"]
    for a, b in ((0, Q // 2), (Q // 2, Q - vx)):
        sget(("qx", a, b), INNER, part("wlist", a, b), ACT.Identity, -4.5, 1.5)
    if vx: vget2(("qx", Q - vx, Q), INNER, part("wlist", Q - vx, Q), 1.5, -4.5, ALU.mult, ALU.add)
    for blk in FINAL:
        term(blk, "id1", "qx")
    mm(full("pl"), full("id1"), full("kt"), True, False)
    for blk in FINAL[:so]:
        sget(reg("qo", blk), ZOUT, wl(blk), ACT.Sign)
    for b, blk in enumerate(FINAL):
        if b >= so:
            vget2(reg("qo", blk), ZOUT, wl(blk), -0.5, 0.5, ALU.max, ALU.min)
        if b in CUT["caps"]:
            x, y = FINAL[CUT["caps"][b][0]][0], FINAL[CUT["caps"][b][1]][1]
            vts(("c_m", x, y), ("c_r", x, y), 2.5, None, ALU.min)
    for b in CUT["ford"]:
        term(FINAL[b], "id1" if b < so else "id2", "qo")
        term(FINAL[b], "idm", "c_m", stop=True)
    FINAL = [FINAL[b] for b in CUT["ford"]]
    for blk in FINAL:
        sact(reg("mag", blk), (blk[2], 0, blk[1] - blk[0]), ACT.Abs, 5.25)
    for blk in FINAL:
        vts(reg("ind", blk), reg("mag", blk), 4.625, 256.0, ALU.is_ge, ALU.mult)
        for a in range(blk[0], blk[1], 128):
            s = 8 * (a // 128 % 2) + a // QP
            mm(full("pl"), ("ind", a, a + 128), ("bh", 15 - s, 143 - s), False, a == FINAL[-1][1] - 128)
    V(lambda: g.vector.tensor_tensor_scan(T.key[:], T.reset[:], T.pl[:, 0:128], 0.0, ALU.add, ALU.min), [full("reset"), full("pl")], [full("key")])
    V(lambda: g.vector.tensor_scalar(T.low[:], T.key[:, 7:128:8], ROUND, -ROUND, ALU.add, ALU.add), [full("key")], [("low", 0, 16)])
    mm(full("pw"), full("key"), full("idq"), True, False, wap=T.key[:, 7:128:8], oap=T.pw[0:16, 0:128])
    mm(full("pk"), ("low", 0, 16), full("ids"), True, True, oap=T.pk[0:16, 0:128])
    mm(full("pw"), ("low", 0, 16), full("idn"), False, True, oap=T.pw[0:16, 0:128])
    S(lambda: g.scalar.activation(T.resc[0:16, :], T.pk[0:16, 0:128], ACT.Identity), [full("pk")], [full("resc")])
    V(lambda: g.vector.tensor_scalar(T.resf[0:16, :], T.pw[0:16, 0:128], 3.5, None, ALU.add), [full("pw")], [full("resf")])
    D("s", lambda: g.scalar.dma_start(T.cost[:], T.resc[0:16, :]), [full("resc")], [])
    D("y", lambda: g.sync.dma_start(T.first[:], T.resf[0:16, :]), [full("resf")], [])
    return ops


def _meet(a, b):
    return a[0] == b[0] and (a[0] in PSUM or (a[1] < b[2] and b[1] < a[2]))


def rank_program(g, core, T, topo):
    rank = T.rank_of(core)
    if rank is None:
        return
    ops = _plan(g, core, T, topo, rank)
    n = len(ops)
    deps = []
    for j in range(n):
        qj, kj, _, rj, wj = ops[j]
        wj2 = wj + [r for r in rj if r[0] in PSUM]
        need = {}
        for i in range(j):
            qi, ki, _, ri, wi = ops[i]
            if qj is None or (qi == "t" and qj == "t") or (qi == "g" and ki[0] == "r"):
                continue
            wi2 = wi + [r for r in ri if r[0] in PSUM]
            if any(_meet(a, b) for a in wi2 for b in rj + wj2) or any(_meet(a, b) for a in ri for b in wj2):
                need[qi if ki == "c" else ("x", i)] = i
        deps.append(need)
    known, after, waits = {}, [None] * n, []
    for j in range(n):
        kn = known.setdefault(ops[j][0], {})
        mine = []
        for key, i in sorted(deps[j].items(), key=lambda t: -t[1]):
            if kn.get(key, -1) >= i:
                continue
            mine.append(i)
            for k2, v2 in after[i].items():
                if kn.get(k2, -1) < v2:
                    kn[k2] = v2
        waits.append(mine)
        mark = dict(kn) if ops[j][0] is not None else {}
        mark[ops[j][0] if ops[j][1] == "c" else ("x", j)] = j
        after[j] = mark
    wanted = set(i for w in waits for i in w)
    queue = {"v": g.vector, "s": g.scalar, "t": g.tensor, "g": g, "y": g.sync}
    csem = {"v": "cv", "s": "cs", "t": "ct", "g": "cg"}
    count, token, ndma = {}, {}, 0
    for j in range(n):
        q, kind, fn, _, _ = ops[j]
        if q is None:
            token[j] = kind
            count[kind[0]] = kind[1]
            continue
        for i in waits[j]:
            queue[q].wait_ge(T.sem[token[i][0]], token[i][1])
        ins = fn()
        if kind == "d":
            name = "d%d" % ndma
            ndma += 1
            ins.then_inc(T.sem[name], 16)
            token[j] = (name, 16)
            count[name] = 16
        elif kind[0] == "r":
            count["sent"] = count.get("sent", 0) + kind[1]
        elif j in wanted:
            count[csem[q]] = count.get(csem[q], 0) + 1
            ins.then_inc(T.sem[csem[q]], 1)
            token[j] = (csem[q], count[csem[q]])
    for name, c in count.items():
        g.wait_ge(T.sem[name], c)
